import numpy as np, ml_dtypes
CORES = [23,119,17,113]
N = 4
BF = ml_dtypes.bfloat16
def gentries(a):
    return np.ascontiguousarray(a.reshape(8, 16, -1).transpose(0, 2, 1)).reshape(8, -1)
def gtable(e):
    e = np.asarray(e); return np.ascontiguousarray(e.reshape(8, -1, 16).transpose(0, 2, 1)).reshape(128, -1).astype(np.int32)
C, D, S, CAP, TH, HOP = 3072, 256, 4, 64, 12, 1
R = C // 16
def inverse(A):
    O = np.zeros_like(A); np.put_along_axis(O, A, np.broadcast_to(np.arange(C), A.shape), -1)
    return O
def estates(A, Y):
    V = np.zeros_like(Y)
    for k in range(16): V += np.take_along_axis(Y, A[:, :, k:k + 1, :], 3)
    return V
def judge(A, O, V, Y, h, z):
    n = h.shape[1]
    ca = np.take_along_axis(A, h[:, None, :], 2)
    yv = np.take_along_axis(Y, ca.reshape(8, 1, 16 * n), 2).reshape(8, 16, 16, n)
    k = np.argmax(np.add.reduce(np.minimum(yv, z[:, :, None, :]), axis=1), axis=1)
    a = np.take_along_axis(ca, k[:, None, :], 1)[:, 0]
    co = np.take_along_axis(O, a[:, None, :], 2)
    vv = np.take_along_axis(V, co.reshape(8, 1, 16 * n), 2).reshape(8, 16, 16, n)
    vc = np.take_along_axis(V, h[:, None, :], 2)
    over = np.add.reduce((vv > vc[:, :, None, :]).astype(np.int64), axis=1)
    j = np.argmax(over, axis=1)[:, None, :]
    return k, a, np.take_along_axis(co, j, 1)[:, 0], np.take_along_axis(over, j, 1)[:, 0]
def meets(x):
    eq = np.any(x[:, None, :, None] == x[None, :, None, :], axis=(2, 3))
    return np.any(np.tril(eq, -1), axis=1)
def exchange(A, O, V, Y, c, f, k, a):
    b = A[k, f]
    ok = ~(meets(np.stack([c, f], 1)) | meets(np.stack([a, b], 1)))
    c, f, k, a, b = c[ok], f[ok], k[ok], a[ok], b[ok]
    A[k, c] = b; A[k, f] = a; O[k, a] = f; O[k, b] = c
    dv = Y[:, b] - Y[:, a]
    V[:, c] += dv; V[:, f] -= dv
def cities(rng):
    rc = np.argsort(rng.random((N, 8, C)), axis=-1); ra = np.argsort(rng.random((N, 8, C)), axis=-1)
    key = rng.random((N, 8, 16, C)); key[:, :, 1:, :R] -= 1.0
    A = np.take_along_axis(ra[:, :, None, :], np.argsort(key, axis=-1), 3)
    A = np.take_along_axis(A, np.argsort(rc, axis=-1)[:, :, None, :], 3)
    m = np.zeros((N, 8, C), bool); np.put_along_axis(m, ra[:, :, :R], True, -1)
    Y = rng.integers(0, 16, (N, 8, 16, C)); Y = np.where(m[:, :, None, :], (Y >> 1) + 8, Y)
    return A, Y, np.ascontiguousarray(rc[:, :, :R])
def duties(rng, rc, n):
    h = np.where(rng.random((N, 8, n)) < 0.125, np.take_along_axis(rc, rng.integers(0, R, (N, 8, n)), 2), rng.integers(0, C, (N, 8, n)))
    top = rng.choice(np.array([0, 1, 3, 7, 7, 11, 15, 15, 15, 15]), (N, 8, 1, n))
    return h, rng.integers(0, top + 1, (N, 8, 16, n))
def ring(rng, A, Y, g, T):
    pc = np.argsort(rng.random((N, C)), axis=-1); pa = np.argsort(rng.random((N, C)), axis=-1)
    for q in range(N):
        A[q, g][:, pc[q]] = pa[q][(np.arange(C)[None, :] + np.arange(16)[:, None]) % C]
        Y[q, g][:, pa[q]] = T[q][:, np.arange(C) % 16]
    return pc
def pack(A, Y, h, z):
    O = inverse(A); V = estates(A, Y)
    w = lambda x: np.ascontiguousarray(x.reshape(N, 128, -1)).astype(np.float32).astype(BF)
    return {"ao": np.ascontiguousarray((A + 4096 * O).reshape(N, 128, C)).astype(np.int32), "yd": w(Y), "ve": w(V), "hd": np.stack([gtable(x) for x in h]), "zc": w(z)}
def setup_inputs(rng):
    A, Y, rc = cities(rng); h, z = duties(rng, rc, D)
    return pack(A, Y, h, z)
def setup_inputs_room(rng):
    A, Y, rc = cities(rng); h4, z4 = duties(rng, rc, 4 * D); O = inverse(A); V = estates(A, Y)
    h = np.zeros((N, 8, D), np.int64); z = np.zeros((N, 8, 16, D), np.int64)
    for q in range(N):
        k, a, f, m = judge(A[q], O[q], V[q], Y[q], h4[q], z4[q]); prop = (m < TH) & (f != h4[q])
        for g in range(8):
            yes = np.nonzero(prop[g])[0]; no = np.nonzero(~prop[g])[0]; ver = np.nonzero(m[g] >= TH)[0]
            if len(yes) == 0: yes = no
            if len(no) == 0: no = yes
            n = int(rng.choice(np.array([0, 1, CAP - 1, CAP, CAP + 1, D])))
            if q == 0: n = (CAP, CAP + 1, D, CAP - 1, 1, 0, CAP, CAP + 1)[g]
            if n == 0 and q % 2 == 0 and len(ver) > 0: no = ver
            ix = rng.permutation(np.concatenate([np.resize(rng.permutation(yes), n), np.resize(rng.permutation(no), D - n)]))
            h[q, g] = h4[q, g, ix]; z[q, g] = z4[q, g][:, ix]
    return pack(A, Y, h, z)
def setup_inputs_clash(rng):
    A, Y, rc = cities(rng); h, z = duties(rng, rc, D); iq = np.arange(N)
    T = rng.integers(0, 11, (N, 16, 16)); w = rng.integers(0, 16, N); T[iq, :, w] = 15
    p2 = ring(rng, A, Y, 2, T)
    T = rng.integers(0, 11, (N, 16, 16)); c4 = rng.integers(0, C, N); ks = np.argsort(rng.random((N, 15)), axis=-1)[:, :2] + 1
    T[iq, :8, (c4 + ks[:, 0]) % 16] = 15; T[iq, 8:, (c4 + ks[:, 1]) % 16] = 15
    p4 = ring(rng, A, Y, 4, T)
    e = int(rng.integers(0, C)); s = int(rng.integers(0, C)); r16 = np.arange(16)
    for q in range(N):
        at = np.argmax(A[q, 6] == s, axis=1); A[q, 6][r16, at] = A[q, 6][r16, e]; A[q, 6][r16, e] = s
    O = inverse(A)
    few = rng.integers(0, C, (N, 8, 24)); hf = np.take_along_axis(few, rng.integers(0, 24, (N, 8, D)), 2)
    st = np.argsort(rng.random((N, 8, C)), axis=-1)[:, :, None, :12]
    own = np.take_along_axis(O, st, 3).reshape(N, 8, 192); ho = np.take_along_axis(own, rng.integers(0, 192, (N, 8, D)), 2)
    Y2 = Y.copy(); np.put_along_axis(Y2, np.broadcast_to(st, (N, 8, 16, 12)), 15, 3)
    Y[:, 1::2] = Y2[:, 1::2]; h[:, ::2] = hf[:, ::2]; h[:, 1::2] = ho[:, 1::2]
    z[:, 1::2] = rng.integers(8, 16, (N, 4, 16, D))
    gap = C // CAP // 16 * 16
    for q in range(N):
        d = rng.permutation(D)[:CAP]; k = rng.integers(1, 16, CAP)
        z[q, 2] = 0; z[q, 2][:, d] = 15; h[q, 2, d] = p2[q, gap * np.arange(CAP) + (w[q] - k) % 16]
    kind = (np.arange(D)[None, :] + rng.integers(0, 2, (N, 1))) % 2
    h[:, 4] = p4[iq, c4][:, None]; z[:, 4] = np.where((np.arange(16) < 8)[None, :, None] == (kind == 0)[:, None, :], 15, 0)
    h[int(rng.integers(0, N)), 6] = e
    return pack(A, Y, h, z)
def setup_inputs_ties(rng):
    A, Y, rc = cities(rng); h, z = duties(rng, rc, D)
    lo = rng.integers(0, 4, (N, 8, 1, 1)); hi = lo + rng.integers(1, 12, (N, 8, 1, 1))
    Y = np.where(rng.random((N, 8, 16, C)) < 0.5, lo, hi)
    z = np.where(rng.random((N, 8, 1, D)) < 0.5, rng.integers(0, 16, (N, 8, 1, D)), z)
    g = rng.permutation(8); Y[:, g[0]] = rng.integers(1, 16, (N, 1, 1)); z[:, g[1]] = 0
    Y[:, g[2]] = rng.integers(14, 16, (N, 16, C)); z[:, g[2]] = np.where(rng.random((N, 1, D)) < 0.5, 15, rng.integers(14, 16, (N, 16, D)))
    return pack(A, Y, h, z)
def setup_inputs_ends(rng):
    A, Y, rc = cities(rng); h, z = duties(rng, rc, D)
    A[:, 1] = np.arange(C); A[:, 2] = (np.arange(C)[None, :] + np.arange(16)[:, None]) % C; A[:, 3] = A[:, 2]
    Y[..., 0] = 15; Y[..., C - 1] = 15; O = inverse(A)
    T = rng.integers(0, 16, (N, 16, 16)); Y[:, 3] = T[:, :, np.arange(C) % 16]
    own = np.ascontiguousarray(O[..., [0, C - 1]]).reshape(N, 8, 32)
    u = rng.random((N, 8, D)); e = rng.choice(np.array([0, C - 1]), (N, 8, D))
    h = np.where(u < 0.4, np.take_along_axis(own, rng.integers(0, 32, (N, 8, D)), 2), np.where(u < 0.5, e, h))
    h[..., 0] = 0; h[..., D - 1] = C - 1
    return pack(A, Y, h, z)
def setup_inputs_spread(rng):
    A, Y, rc = cities(rng); h, z = duties(rng, rc, D)
    s = np.exp2(4 * rng.random((N, 8, 1, C))) * np.exp2(-2 * rng.random((N, 8, 16, 1)))
    Y = np.minimum((s * rng.random((N, 8, 16, C))).astype(np.int64), 15)
    Y[rng.random(Y.shape) < 0.05] = 15
    z = np.minimum((np.exp2(5 * rng.random((N, 8, 1, D))) * rng.random((N, 8, 16, D))).astype(np.int64), 15)
    return pack(A, Y, h, z)
def check_inputs(d):
    bad = []
    for k, hi in (("yd", 15), ("zc", 15), ("ve", 240)):
        x = np.asarray(d[k]).astype(np.float32)
        if not np.all((x >= 0) & (x <= hi) & (x == np.floor(x))): bad.append("range of " + k)
    if np.min(d["hd"]) < 0 or np.max(d["hd"]) > C - 1: bad.append("range of hd")
    ao = np.asarray(d["ao"]).astype(np.int64).reshape(N, 8, 16, C); A = ao & 4095; O = ao >> 12
    if np.min(ao) < 0 or np.max(A) > C - 1 or np.max(O) > C - 1: return bad + ["range of ao"]
    m = np.zeros(A.shape, bool); np.put_along_axis(m, A, True, -1)
    if not np.all(m): bad.append("a row of A is no permutation")
    if not np.all(np.take_along_axis(O, A, 3) == np.arange(C)): bad.append("O is not the inverse of A")
    if not bad:
        Y = np.asarray(d["yd"]).astype(np.float32).astype(np.int64).reshape(N, 8, 16, C)
        if not np.all(estates(A, Y) == np.asarray(d["ve"]).astype(np.float32).astype(np.int64).reshape(N, 8, 16, C)): bad.append("ve is not the sum of the yields")
    return bad
def reference(ao, yd, ve, hd, zc):
    w = ao.astype(np.int64).reshape(N, 8, 16, C); A = w & 4095; O = w >> 12
    Y = yd.astype(np.float32).astype(np.int64).reshape(N, 8, 16, C); V = ve.astype(np.float32).astype(np.int64).reshape(N, 8, 16, C)
    z = zc.astype(np.float32).astype(np.int64).reshape(N, 8, 16, D); h = np.stack([gentries(x) for x in hd]).astype(np.int64)
    log = []
    for t in range(S):
        new = []
        for q in range(N):
            k, a, f, m = judge(A[q], O[q], V[q], Y[q], h[q], z[q])
            for g in range(8):
                ix = np.nonzero((m[g] < TH) & (f[g] != h[q, g]))[0][:CAP]
                exchange(A[q, g], O[q, g], V[q, g], Y[q, g], h[q, g, ix], f[g, ix], k[g, ix], a[g, ix])
            new.append(np.where(m >= TH, f, h[q]))
        h = np.stack(new); log.append(h)
        if t < S - 1:
            h = np.roll(h, HOP, axis=0); z = np.roll(z, HOP, axis=0)
    return {"vo": V.reshape(N, 128, C).astype(np.float32).astype(BF), "ho": np.stack(log, axis=2).reshape(N, 8, S * D).astype(np.float32)}

@@ -1,0 +1,490 @@
+import numpy as np
+from concourse.mybir import AluOpType as ALU, ActivationFunctionType as AF
+
+N, C, D, S, HOP = 4, 3072, 256, 4, 1
+PAD = 2 * C
+V1, V2 = 192, 160
+VOH = 11
+MAGIC = 1.5 * 2.0 ** 35
+F, B, H, I32, U16 = "float32", "bfloat16", "float16", "int32", "uint16"
+SCRATCH = {}
+for _n, _w, _d in (
+        ("aoraw", C, I32), ("AO", PAD + 256, I32), ("VY", PAD + 256, B), ("z0", D, B), ("zin", 3 * D, B),
+        ("z16a", 16 * D, B), ("z16b", 16 * D, B), ("mn", 16 * D, B), ("gy", 1536, B), ("vc", D, B), ("vcx", 16 * D, B),
+        ("hdi", 16, I32), ("hdo", 16, F), ("hl0", 16, U16), ("hin", 96, U16), ("hsend", 96, U16),
+        ("ca", D, U16), ("cah", D, H), ("sc", D, F), ("rn", 16, F), ("af", 16, F), ("bi", 16, I32), ("ki", 16, I32),
+        ("TM", D, H), ("la", 16, U16), ("hT", 16, F), ("hn", 16, F), ("ver", 16, F), ("nz", 16, F), ("prop", 16, B), ("df", 16, F), ("rp", 16, F),
+        ("vz", 2304, H), ("oh", 1024, B), ("sq", 1280, F), ("rs16", 64, H), ("rb16", 64, H), ("LM", D, F), ("LS", D, F), ("gl", 16, U16),
+        ("K64", 64, F), ("prod", 64, F), ("E", 1280, B), ("KD", D, F), ("NW", D, I32), ("vg", D, B), ("nv", 128, B),
+        ("PM", D, F), ("PS", D, F), ("of", 16, F), ("so", 16, U16), ("hob", 512, F),
+        ("ipi", 1, I32), ("ip", 1, F), ("p16i", 1, I32), ("pgi", 1, I32), ("p16", 1, F), ("pg", 1, F), ("kcode", 1, F), ("sv", 16, F), ("ub", 1, F),
+        ("i128", 128, F), ("imod", D, F), ("idiv", 128, F), ("ipad", D, F),
+        ("If", 128, F), ("Ib", 128, B), ("Inb", 128, B), ("U", 128, B), ("on", 128, B), ("m256", D, F), ("bo", 128, F),
+        ("boh", 128, B), ("jj", 8, B), ("blk", 8, B), ("nblk", 8, B), ("zblk", 128, B), ("rst", D, F), ("brow", 128, B),
+        ("io64", 64, B), ("exl", 8, U16), ("mk", 64, B), ("mkb", 64, B), ("DP", D, F), ("k8192", 64, B), ("k3072", 64, B),
+        ("se0", 128, B), ("se2", 128, B), ("se3", 128, B), ("se4n", 128, B), ("se0n", 128, B), ("se2n", 128, B),
+        ("sd", 128, B), ("sdn", 128, B), ("sb0", 128, B), ("sb1", 128, B), ("sb2", 128, B)):
+    SCRATCH[_n] = ("sbuf", [128, _w], _d)
+for _i in range(8):
+    SCRATCH["P%d" % _i] = ("psum", [128, 512], F)
+SEMAPHORES = ["cV", "cA", "cP", "cG"] + ["d%d" % i for i in range(24)] + ["az1", "az2", "az3", "ah1", "ah2", "ah3", "lz", "lh"]
+
+
+def rank_program(g, core, T, topo):
+    rank = T.rank_of(core)
+    if rank is None:
+        return
+    Q = {"V": g.vector, "A": g.scalar, "P": g.tensor, "G": g, "S": g.sync}
+    cnt = {}
+    seen = {q: {} for q in Q}
+    snap = {}
+    Wr, Rd = {}, {}
+    toks = [None]
+
+    def new_token(q, sem, n):
+        cnt[sem] = cnt.get(sem, 0) + n
+        toks.append((sem, cnt[sem], q))
+        snap[len(toks) - 1] = dict(seen[q])
+        return len(toks) - 1
+
+    def wait_tok(q, i):
+        sem, v, _ = toks[i]
+        if seen[q].get(sem, 0) >= v:
+            return
+        Q[q].wait_ge(T.sem[sem], v)
+        seen[q][sem] = v
+        for s2, v2 in snap[i].items():
+            if v2 > seen[q].get(s2, 0):
+                seen[q][s2] = v2
+
+    def track(name):
+        if name not in Wr:
+            Wr[name] = np.zeros(SCRATCH[name][1][1], np.int64)
+            Rd[name] = {}
+
+    def need(q, reads, writes):
+        ids = set()
+        for kind, accs in ((0, reads), (1, writes)):
+            for name, cols in accs:
+                track(name)
+                if SCRATCH[name][0] == "psum":
+                    for arr in list(Rd[name].values()) + [Wr[name]]:
+                        ids.update(int(x) for x in np.unique(arr) if x and toks[int(x)][2] != q)
+                else:
+                    ids.update(int(x) for x in np.unique(Wr[name][cols]))
+                    if kind:
+                        for arr in Rd[name].values():
+                            ids.update(int(x) for x in np.unique(arr[cols]))
+        ids.discard(0)
+        if q == "P":
+            ids = {i for i in ids if toks[i][0] != "cP"}
+        for i in sorted(ids, reverse=True):
+            wait_tok(q, i)
+
+    def note(tok, reads, writes):
+        key = toks[tok][0]
+        for name, cols in reads:
+            Rd[name].setdefault(key, np.zeros(len(Wr[name]), np.int64))[cols] = tok
+        for name, cols in writes:
+            Wr[name][cols] = tok
+
+    def op(q, call, writes, reads):
+        rr = [a for x in reads for a in x[1]]
+        ww = [a for x in writes for a in x[1]]
+        need(q, rr, ww)
+        call().then_inc(T.sem["c" + q], 1)
+        note(new_token(q, "c" + q, 1), rr, ww)
+
+    def X(name, a=None, b=None, s=1, p=None):
+        a = 0 if a is None else a
+        b = SCRATCH[name][1][1] if b is None else b
+        ps = slice(None) if p is None else slice(p[0], p[1])
+        ap = T[name][ps, a:b] if s == 1 else T[name][ps, a:b:s]
+        return (ap, [(name, np.arange(a, b, s))])
+
+    def IND(win, off):
+        return (win[0].indirect(off[0]), win[1] + off[1])
+
+    def cp(o, i):
+        op("V", lambda: g.vector.tensor_copy(o[0], i[0]), [o], [i])
+
+    def tt(o, a, b, f):
+        op("V", lambda: g.vector.tensor_tensor(o[0], a[0], b[0], f), [o], [a, b])
+
+    def val(x, rs):
+        if isinstance(x, tuple):
+            rs.append(x)
+            return x[0]
+        return x
+
+    def ts(o, a, s1, f1, s2=None, f2=None):
+        rs = [a]
+        v1, v2 = val(s1, rs), val(s2, rs)
+        if f2 is None:
+            op("V", lambda: g.vector.tensor_scalar(o[0], a[0], v1, None, f1), [o], rs)
+        else:
+            op("V", lambda: g.vector.tensor_scalar(o[0], a[0], v1, v2, f1, f2), [o], rs)
+
+    def scan(o, d0, d1, f1):
+        op("V", lambda: g.vector.tensor_tensor_scan(o[0], d0[0], d1[0], 0.0, ALU.mult, f1), [o], [d0, d1])
+
+    def act(o, i, f=AF.Copy, bias=0.0, scale=1.0):
+        rs = [i]
+        b, c = val(bias, rs), val(scale, rs)
+        op("A", lambda: g.scalar.activation(o[0], i[0], f, bias=b, scale=c), [o], rs)
+
+    def mm(o, l, r, start, stop):
+        op("P", lambda: g.tensor.matmul(o[0], l[0], r[0], start, stop), [o], [l, r])
+
+    def iota(o, pat, base, cm):
+        if SCRATCH[o[1][0][0]][2] == I32:
+            op("G", lambda: g.iota(o[0], pat, base, cm), [o], [])
+        else:
+            op("G", lambda: g.iota(o[0], pat, base, cm, allow_small_or_imprecise_dtypes=True), [o], [])
+
+    nd = [0]
+
+    def dma(q, o, i):
+        need(q, i[1], o[1])
+        sem = "d%d" % nd[0]
+        nd[0] += 1
+        Q[q].dma_start(o[0], i[0]).then_inc(T.sem[sem], 16)
+        note(new_token(q, sem, 16), i[1], o[1])
+
+    def send(dst, name, a, b, name2, a2, rsem, lsem):
+        src = X(name, a, b)
+        need("G", src[1], [])
+        rid, pid, _ = topo.addr(dst)
+        eng = topo.engines(core, dst)[:8]
+        g.remote_dma(T[name2][:, a2:a2 + b - a], src[0], T.sem[rsem], T.sem[lsem], pid, rid, sum(1 << e for e in eng))
+        note(new_token("G", lsem, len(eng)), src[1], [])
+
+    def arrives(name, a, b, rsem, src):
+        track(name)
+        cnt[rsem] = len(topo.engines(src, core)[:8])
+        toks.append((rsem, cnt[rsem], "R"))
+        snap[len(toks) - 1] = {}
+        Wr[name][a:b] = len(toks) - 1
+
+    EQ, MU, AD, SU = ALU.is_equal, ALU.mult, ALU.add, ALU.subtract
+    dma("S", X("hdi"), (T.hd[:, :], []))
+    dma("A", X("z0"), (T.zc[:, :], []))
+    w = C // 4
+    for i in range(4):
+        dma("SA"[i % 2], X("aoraw", i * w, i * w + w), (T.ao[:, i * w:i * w + w], []))
+    dma("S", X("VY", C, C + C // 2), (T.yd[:, 0:C // 2], []))
+    dma("A", X("VY", C + C // 2, PAD), (T.yd[:, C // 2:C], []))
+    dma("S", X("VY", 0, C // 2), (T.ve[:, 0:C // 2], []))
+    dma("A", X("VY", C // 2, C), (T.ve[:, C // 2:C], []))
+    iota(X("ipi"), [[0, 1]], 0, 1)
+    iota(X("ip"), [[0, 1]], 0, 1)
+    iota(X("i128"), [[1, 128]], 0, 0)
+    iota(X("imod"), [[0, 16], [1, 16]], 0, 0)
+    iota(X("idiv"), [[1, 8], [0, 16]], 0, 0)
+    iota(X("on"), [[0, 128]], 1, 0)
+    iota(X("ipad"), [[1, 256]], PAD, 0)
+    iota(X("io64"), [[1, 64]], 1, 0)
+    iota(X("mk", 16, 64), [[0, 48]], 0, 0)
+    iota(X("mkb", 16, 64), [[0, 48]], 4608, 0)
+    iota(X("k8192"), [[0, 64]], 8192, 0)
+    iota(X("k3072"), [[0, 64]], 3072, 0)
+    for r in range(1, N):
+        send(T.cores[(rank + r * HOP) % N], "z0", 0, D, "zin", (r - 1) * D, "az%d" % r, "lz")
+        arrives("zin", (r - 1) * D, r * D, "az%d" % r, T.cores[(rank - r * HOP) % N])
+        arrives("hin", (r - 1) * 32, r * 32, "ah%d" % r, T.cores[(rank - HOP) % N])
+    p, p16, pg = X("ip"), X("p16"), X("pg")
+    ts(X("p16i"), X("ipi"), 15, ALU.bitwise_and)
+    ts(X("pgi"), X("ipi"), 4, ALU.logical_shift_right)
+    ts(X("If"), X("i128"), p, EQ)
+    cp(X("p16"), X("p16i"))
+    cp(X("pg"), X("pgi"))
+    ts(X("vz", 0, 256), X("imod"), 0.0, MU)
+    cp(X("vz", 256, 512), X("vz", 0, 256))
+    cp(X("vz", 512, 1024), X("vz", 0, 512))
+    cp(X("vz", 1024, 2048), X("vz", 0, 1024))
+    cp(X("vz", 2048, 2304), X("vz", 0, 256))
+    ts(X("vz", 4, 2165, 144), X("imod", 0, 16), 0.0, MU, 1.0, AD)
+    cp(X("hl0"), X("hdi"))
+    ts(X("hdo"), X("hdi"), -1536.0, AD)
+    ts(X("jj"), X("i128", 0, 8), pg, EQ)
+    ts(X("bo"), X("idiv"), pg, EQ)
+    cp(X("exl"), X("i128", 0, 8))
+    ts(X("m256"), X("imod"), p16, EQ)
+    sv = lambda i: X("sv", i, i + 1)
+    for v in range(4):
+        ts(sv(v), p16, float(v), EQ)
+    for i, c in ((4, -8192.0), (5, 1536.0), (6, 4608.0)):
+        ts(sv(i), p16, 4.0, EQ, c, MU)
+    tt(sv(8), sv(0), sv(5), AD)
+    tt(sv(9), sv(1), sv(5), AD)
+    tt(sv(10), sv(2), sv(6), AD)
+    tt(sv(11), sv(1), sv(0), SU)
+    ts(X("mk", 0, 16), X("imod", 0, 16), p16, ALU.is_le, 16384.0, MU)
+    act(X("Ib"), X("If"))
+    act(X("Inb"), X("If"), scale=-1.0)
+    act(X("brow"), X("imod", 0, 128), bias=61440.0, scale=-4096.0)
+    act(X("rst"), X("imod"), AF.Sign)
+    act(X("ub"), p, bias=100.0, scale=-200.0)
+    act(X("U"), X("i128"), AF.Sigmoid, X("ub"), 200.0)
+    for k in range(16):
+        act(X("z16a", k, 16 * D, 16), X("z0"))
+    act(X("blk"), X("jj"), scale=65536.0)
+    act(X("nblk"), X("jj"), scale=-65536.0)
+    bo = X("bo")
+    act(X("zblk"), bo, scale=65536.0)
+    act(X("boh"), bo, scale=8192.0)
+    act(X("kcode"), p16, bias=15.0, scale=-1.0)
+    act(X("mkb", 0, 16), X("mk", 0, 16), bias=4608.0)
+    for nm, v in (("se0", 0), ("se2", 2), ("se3", 3), ("se4n", 4), ("sb0", 8), ("sb1", 9), ("sb2", 10), ("sd", 11)):
+        act(X(nm), bo, scale=sv(v))
+    for nm, src in (("se0n", "se0"), ("se2n", "se2"), ("sdn", "sd")):
+        act(X(nm), X(src), scale=-1.0)
+    blocks = []
+    o = 0
+    for q in range(4):
+        blocks.append((o, 64 - 16 * q))
+        o += 2 * (64 - 16 * q)
+    for i in range(4):
+        ts(X("AO", i * w, i * w + w), X("aoraw", i * w, i * w + w), 4095, ALU.bitwise_and)
+
+    half = lambda nm, hf: X(nm, 8 * hf, 8 * hf + 8)
+
+    def conv_a(nm, hf):
+        tt(X("TM", 128 * hf, 128 * hf + 128), IND(half(nm, hf), X("exl")), X("m256", 128 * hf, 128 * hf + 128), MU)
+
+    def conv_b(out, hf):
+        mm(out, X("TM", 128 * hf, 128 * hf + 128), X("jj"), True, True)
+
+    lists = lambda hf: X("P2" if hf == 0 else "P3", 384, 392)
+
+    def embed():
+        for hf in range(2):
+            mm(X("P%d" % hf, 0, 128), X("cah", 128 * hf, 128 * hf + 128), X("Ib"), True, False)
+
+    def reduce(d0, d1, w):
+        hf, b = d0 // 128, d0 % 128
+        for k in range(16):
+            mm(X("P%d" % hf, k, 128, 16, (b, b + d1 - d0)), X("mn", 16 * d0 + k, 16 * d1, 16), X(w), False, False)
+
+    def close(hf):
+        mm(X("P%d" % hf, 0, 128), X("on", p=(0, 1)), X("brow", p=(0, 1)), False, True)
+
+    def best_of(hf):
+        scan(X("sc", 128 * hf, 128 * hf + 128), X("rst", 0, 128), X("P%d" % hf, 0, 128), ALU.max)
+
+    best = X("sc", 15, 256, 16)
+    bst = lambda hf: X("sc", 128 * hf + 15, 128 * hf + 128, 16)
+    for t in range(S):
+        last = t == S - 1
+        hl = X("hl0") if t == 0 else X("hin", (t - 1) * 32, (t - 1) * 32 + 16)
+        zrow = X("z0", V1, D) if t == 0 else X("zin", (t - 1) * D + V1, t * D)
+        z16 = ("z16a", "z16b")[t % 2]
+        if not last:
+            for k in range(16):
+                zo, zi = X(("z16a", "z16b")[(t + 1) % 2], k, 16 * D, 16), X("zin", t * D, t * D + D)
+                op("G", lambda: g.affine_select(zo[0], zi[0], [[0, D]], ALU.is_ge, 0.0, 0, 0), [zo], [zi])
+        for i, d0 in enumerate(range(V1, D, 32)):
+            mm(X("P%d" % (3 + i)), X("Ib"), X(z16, 16 * d0, 16 * d0 + 512), True, False)
+        cp(X("ca"), IND(X("AO", 0, C), hl))
+        ts(X("cah"), X("ca"), -1536.0, AD)
+        embed()
+        mm(X("P1", 0, 128, 1, (64, 128)), zrow, X("zblk"), False, False)
+
+        def vmin(a, b):
+            tt(X("mn", 16 * a, 16 * b), IND(X("VY", C, PAD), X("ca", a, b)), X(z16, 16 * a, 16 * b), ALU.min)
+        if t == 0:
+            for i in range(4):
+                ts(X("AO", C + i * w, C + i * w + w), X("aoraw", i * w, i * w + w), 12, ALU.logical_shift_right)
+        vmin(0, 128)
+        for i, d0 in enumerate(range(V1, D, 32)):
+            act(X("gy", 512 * i, 512 * i + 512), IND(X("VY", C, PAD), X("ca", d0, d0 + 32)))
+            mm(X("P%d" % (3 + i)), X("Inb"), X("gy", 512 * i, 512 * i + 512), False, True)
+        for i, d0 in enumerate(range(V1, D, 32)):
+            act(X("mn", 16 * d0, 16 * d0 + 512), X("P%d" % (3 + i)), AF.Relu)
+        act(X("vc"), IND(X("VY", 0, C), hl))
+        for j in range(16):
+            act(X("vcx", j, 16 * D, 16), X("vc"))
+        reduce(V1, V1 + 32, "nblk")
+        reduce(0, 128, "blk")
+        close(0)
+        vmin(128, 160)
+        reduce(128, 160, "blk")
+        vmin(160, V1)
+        reduce(V1 + 32, D, "nblk")
+        reduce(160, V1, "blk")
+        close(1)
+        if t == 0:
+            for hf in range(2):
+                conv_a("hdo", hf)
+                conv_b(lists(hf), hf)
+                cp(half("hT", hf), lists(hf))
+        else:
+            ts(X("hT"), X("hin", (t - 1) * 32 + 16, t * 32), -1536.0, AD)
+        cp(X("vz", 0, 2161, 144), X("hT"))
+        best_of(0)
+        ts(half("rn", 0), bst(0), MAGIC, AD, MAGIC, SU)
+        tt(half("af", 0), bst(0), half("rn", 0), SU)
+        best_of(1)
+        conv_a("af", 0)
+        ts(half("rn", 1), bst(1), MAGIC, AD, MAGIC, SU)
+        conv_b(lists(0), 0)
+        cp(X("vz", 2, 1011, 144), half("af", 0))
+        tt(half("af", 1), bst(1), half("rn", 1), SU)
+        ts(half("la", 0), lists(0), 1536.0, AD)
+        conv_a("af", 1)
+        conv_b(lists(1), 1)
+        cp(X("ca", 0, 128), IND(X("AO", C, PAD), half("la", 0)))
+        ts(half("la", 1), lists(1), 1536.0, AD)
+        cp(X("vz", 1154, 2163, 144), half("af", 1))
+        cp(X("ca", 128, 256), IND(X("AO", C, PAD), half("la", 1)))
+        ts(X("bi"), X("rn"), 1.0 / 4096, MU)
+        for i, d0 in enumerate(range(V2, D, 32)):
+            mm(X("P%d" % (5 + i)), X("Inb"), X("vcx", 16 * d0, 16 * d0 + 512), True, False)
+
+        def vgt(a, b):
+            tt(X("mn", 16 * a, 16 * b), IND(X("VY", 0, C), X("ca", a, b)), X("vcx", 16 * a, 16 * b), ALU.is_gt)
+        ts(X("cah"), X("ca"), -1536.0, AD)
+        vgt(0, 128)
+        for i, d0 in enumerate(range(V2, D, 32)):
+            act(X("gy", 512 * i, 512 * i + 512), IND(X("VY", 0, C), X("ca", d0, d0 + 32)))
+            mm(X("P%d" % (5 + i)), X("Ib"), X("gy", 512 * i, 512 * i + 512), False, True)
+        for i, d0 in enumerate(range(V2, D, 32)):
+            act(X("mn", 16 * d0, 16 * d0 + 512), X("P%d" % (5 + i)), AF.Sigmoid, -100.0, 200.0)
+        ts(X("ki"), X("bi"), 15, ALU.bitwise_and)
+        vgt(128, V2)
+        cp(X("vz", 3, 2164, 144), X("ki"))
+        embed()
+        reduce(0, 128, "blk")
+        close(0)
+        reduce(128, 256, "blk")
+        close(1)
+        if t == 0:
+            tt(X("DP"), X("m256"), X("ipad"), MU)
+        best_of(0)
+        best_of(1)
+        ts(X("rn"), best, MAGIC, AD, MAGIC, SU)
+        ts(X("ver"), best, 12.0 * 65536 - 1536, ALU.is_ge)
+        tt(X("af"), best, X("rn"), SU)
+        tt(X("nz"), X("af"), X("hT"), ALU.not_equal)
+        tt(X("df"), X("af"), X("hT"), SU)
+        tt(X("prop"), X("nz"), X("ver"), ALU.is_gt)
+        cp(X("vz", 1, 2162, 144), X("af"))
+        mm(X("P2", 144, 152), X("U"), X("prop", 0, 8), True, True)
+        mm(X("P2", 152, 160), X("U"), X("prop", 8, 16), True, False)
+        mm(X("P2", 152, 160), X("on"), X("prop", 0, 8), False, True)
+        tt(X("rp"), X("P2", 144, 160), X("prop"), MU)
+        for i in range(VOH, 16):
+            act(X("sq", 64 * (i - VOH), 64 * (i - VOH) + 64), X("io64"), AF.Square, X("rp", i, i + 1), -1.0)
+        for i in range(VOH, 16):
+            act(X("oh", 64 * i, 64 * i + 64), X("sq", 64 * (i - VOH), 64 * (i - VOH) + 64), AF.Relu, 1.0, -1.0)
+        for i in range(16):
+            if i < VOH:
+                ts(X("oh", 64 * i, 64 * i + 64), X("io64"), X("rp", i, i + 1), EQ)
+            hf, gg = i // 8, i % 8
+            mm(X("P2", 0, 64), X("vz", 128 * gg + 1152 * hf, 128 * gg + 1152 * hf + 128), X("oh", 64 * i, 64 * i + 64), i == 0, i == 15)
+        tt(X("df"), X("df"), X("ver"), MU)
+        cp(X("rs16"), X("P2", 0, 64))
+        tt(X("hn"), X("df"), X("hT"), AD)
+        for v, nm in enumerate(("sb0", "sb1", "sb2", "se3")):
+            mm(X("P3", 64 * v, 64 * v + 64), X(nm), X("rs16"), True, True)
+        mm(X("P2", 64, 128), X("Ib"), X("k3072"), True, False)
+
+        def rows(bank, q, hh, nm, src, m):
+            o, wd = blocks[q]
+            mm(X(bank, o + hh * wd, o + hh * wd + wd), X("Ib"), X(m, 0, wd), True, False)
+            mm(X(bank, o + hh * wd, o + hh * wd + wd), X(nm), X(src, 16 * q, 64), False, True)
+        for q in range(4):
+            rows("P4", q, 0, "sb0", "rs16", "mk")
+            rows("P4", q, 1, "sb1", "rs16", "mk")
+        tt(X("LM", 0, 192), X("P3", 0, 192), X("m256", 0, 192), MU)
+        ts(X("K64"), X("P3", 192, 256), X("kcode"), EQ)
+        scan(X("LS", 0, 192), X("rst", 0, 192), X("LM", 0, 192), AD)
+        cp(X("gl", 0, 12), X("LS", 15, 192, 16))
+        tt(X("prod"), IND(X("AO", 0, C), X("gl", 4, 8)), X("K64"), MU)
+        mm(X("P2", 64, 128), bo, X("prod"), False, True)
+        for q in range(4):
+            rows("P5", q, 0, "sb2", "rs16", "mk")
+        if not last:
+            conv_a("hn", 0)
+            conv_a("hn", 1)
+            ts(X("hsend", 32 * t + 16, 32 * t + 32), X("hn"), 1536.0, AD)
+        ts(X("rb16"), X("P2", 64, 128), -4608.0, AD)
+        tt(X("LM", 192, 256), X("P2", 64, 128), X("m256", 0, 64), MU)
+        scan(X("LS", 192, 256), X("rst", 0, 64), X("LM", 192, 256), AD)
+        cp(X("gl", 12, 16), X("LS", 207, 256, 16))
+        for q in range(4):
+            rows("P5", q, 1, "se0", "rb16", "mkb")
+        if not last:
+            for hf in range(2):
+                conv_b(X("P2", 128 + 8 * hf, 136 + 8 * hf), hf)
+            ts(X("hsend", 32 * t, 32 * t + 16), X("P2", 128, 144), 1536.0, AD)
+            send(T.cores[(rank + HOP) % N], "hsend", 32 * t, 32 * t + 32, "hin", 32 * t, "ah%d" % (t + 1), "lh")
+            mm(X("P6", 0, 64), X("se0"), X("rb16"), True, False)
+            mm(X("P6", 0, 64), X("se2n"), X("rs16"), False, True)
+            mm(X("P6", 64, 128), X("se0n"), X("rb16"), True, False)
+            mm(X("P6", 64, 128), X("se2"), X("rs16"), False, True)
+            mm(X("P6", 128, 192), X("sd"), X("rs16"), True, True)
+            mm(X("P6", 192, 256), X("sdn"), X("rs16"), True, True)
+        mm(X("P7", 0, 64), X("Ib"), X("k8192"), True, False)
+        mm(X("P7", 0, 64), X("se4n"), X("rs16"), False, False)
+        pr = {}
+        e = 0
+        for bank, base in (("P4", 0), ("P5", 128)):
+            for q in range(4):
+                o, wd = blocks[q]
+                for v in range(2):
+                    ls = base + 64 * v + 16 * q + 15
+                    pr[bank, q, v] = (X(bank, o, o + 2 * wd), X("LS", ls, ls + 1), e, wd)
+                    e += 2 * wd
+
+        def count(key, fin=False):
+            _, _, e, wd = pr[key]
+            for hh in range(2):
+                mm(X("P7", 64 - wd, 64), X("boh"), X("E", e + hh * wd, e + hh * wd + wd), False, fin and hh == 1)
+
+        def by_scalar(keys):
+            for key in keys:
+                src, col, e, wd = pr[key]
+                act(X("sq", e, e + 2 * wd), src, AF.Square, col, -1.0)
+            for key in keys:
+                src, col, e, wd = pr[key]
+                act(X("E", e, e + 2 * wd), X("sq", e, e + 2 * wd), AF.Relu, 1.0, -1.0)
+                count(key)
+
+        def by_vector(key):
+            src, col, e, wd = pr[key]
+            ts(X("E", e, e + 2 * wd), src, col, EQ)
+        by_scalar([("P4", q, v) for q in range(4) for v in range(2)])
+        by_scalar([("P5", q, v) for q in (2, 3) for v in range(2)])
+        act(X("vg"), IND(X("VY", 0, PAD), X("gl")))
+        for q in (1, 0):
+            for v in range(2):
+                by_vector(("P5", q, v))
+                count(("P5", q, v), q == 0 and v == 1)
+        for o, ya, yb in ((0, "Inb", "Ib"), (64, "Ib", "Inb")):
+            mm(X("P3", 256 + o, 320 + o), X("Ib"), X("vg", o, o + 64), True, False)
+            mm(X("P3", 256 + o, 320 + o), X(ya), X("vg", 128, 192), False, False)
+            mm(X("P3", 256 + o, 320 + o), X(yb), X("vg", 192, 256), False, True)
+        act(X("nv"), X("P3", 256, 384))
+        mm(X("P2", 160, 288, 1, (0, 16)), X("hn"), X("If"), True, True)
+        act(X("hob", 128 * t, 128 * t + 128, 1, (0, 16)), X("P2", 160, 288, 1, (0, 16)), AF.Copy, 1536.0)
+        if not last:
+            for v in range(4):
+                tt(X("KD", 64 * v, 64 * v + 64), X("P6", 64 * v, 64 * v + 64), X("K64"), MU)
+            tt(X("NW"), IND(X("AO", 0, PAD), X("gl")), X("KD"), AD)
+        nq = 2 if last else 4
+        for v in range(nq):
+            tt(X("PM", 64 * v, 64 * v + 64), X("P7", 0, 64), X("DP", 64 * v, 64 * v + 64), ALU.min)
+        scan(X("PS", 0, 64 * nq), X("rst", 0, 64 * nq), X("PM", 0, 64 * nq), AD)
+        tt(X("of", 0, 4 * nq), X("PS", 15, 64 * nq, 16), X("LS", 15, 64 * nq, 16), ALU.max)
+        cp(X("so", 0, 4 * nq), X("of", 0, 4 * nq))
+        if not last:
+            cp(IND(X("AO"), X("so")), X("NW"))
+        cp(IND(X("VY"), X("so", 0, 8)), X("nv"))
+        for hf in range(2):
+            c0 = t * D + hf * 128
+            dma("S", (T.ho[:, c0:c0 + 128], []), X("hob", 128 * t, 128 * t + 128, 1, (8 * hf, 8 * hf + 8)))
+    dma("S", (T.vo[:, :], []), X("VY", 0, C))
+    for sem, v in sorted(cnt.items()):
+        if seen["G"].get(sem, 0) < v:
+            g.wait_ge(T.sem[sem], v)

@@ -2,32 +2,38 @@ import numpy as np
 from concourse.mybir import AluOpType as ALU, ActivationFunctionType as AF
 
 N, C, D, S, HOP = 4, 3072, 256, 4, 1
-PAD = 2 * C
-V1, V2 = 192, 160
-VOH = 11
+NA = ((48, 80), (80, 48))
+CUTS = (((0, 128), (0, 128)), ((0, 128), (0, 128)))
+VCHUNK = 32
+CASPLIT = 1
+AOH = 0
+APAIR, BPAIR, RELU = 6, 0, 256
+GZ, GVC = 16, (10, 8)
+TURN = dict(ca=(0, 1), s1=(4, 5), d1=(6, 9), s2=(12, 14), d2=(12, 17), vg=9, vc=(10, 13), vt=102, upd=107, k=15, hn=26, ho=68, x=25, nw=26, zx=73)
+AHEAD, PAHEAD, SLACK, ROUNDS = 0.1, 0.0, 0.02, 2
 MAGIC = 1.5 * 2.0 ** 35
+CYC, PECYC, WAKE, GATHER, SCATTER, HOPTIME, LOADRATE = 0.9e-3, 0.65e-3, 0.13, 1.56, 3.8, 2.5, 250e3
 F, B, H, I32, U16 = "float32", "bfloat16", "float16", "int32", "uint16"
 SCRATCH = {}
 for _n, _w, _d in (
-        ("aoraw", C, I32), ("AO", PAD + 256, I32), ("VY", PAD + 256, B), ("z0", D, B), ("zin", 3 * D, B),
-        ("z16a", 16 * D, B), ("z16b", 16 * D, B), ("mn", 16 * D, B), ("gy", 1536, B), ("vc", D, B), ("vcx", 16 * D, B),
-        ("hdi", 16, I32), ("hdo", 16, F), ("hl0", 16, U16), ("hin", 96, U16), ("hsend", 96, U16),
-        ("ca", D, U16), ("cah", D, H), ("sc", D, F), ("rn", 16, F), ("af", 16, F), ("bi", 16, I32), ("ki", 16, I32),
-        ("TM", D, H), ("la", 16, U16), ("hT", 16, F), ("hn", 16, F), ("ver", 16, F), ("nz", 16, F), ("prop", 16, B), ("df", 16, F), ("rp", 16, F),
-        ("vz", 2304, H), ("oh", 1024, B), ("sq", 1280, F), ("rs16", 64, H), ("rb16", 64, H), ("LM", D, F), ("LS", D, F), ("gl", 16, U16),
-        ("K64", 64, F), ("prod", 64, F), ("E", 1280, B), ("KD", D, F), ("NW", D, I32), ("vg", D, B), ("nv", 128, B),
-        ("PM", D, F), ("PS", D, F), ("of", 16, F), ("so", 16, U16), ("hob", 512, F),
-        ("ipi", 1, I32), ("ip", 1, F), ("p16i", 1, I32), ("pgi", 1, I32), ("p16", 1, F), ("pg", 1, F), ("kcode", 1, F), ("sv", 16, F), ("ub", 1, F),
-        ("i128", 128, F), ("imod", D, F), ("idiv", 128, F), ("ipad", D, F),
-        ("If", 128, F), ("Ib", 128, B), ("Inb", 128, B), ("U", 128, B), ("on", 128, B), ("m256", D, F), ("bo", 128, F),
-        ("boh", 128, B), ("jj", 8, B), ("blk", 8, B), ("nblk", 8, B), ("zblk", 128, B), ("rst", D, F), ("brow", 128, B),
-        ("io64", 64, B), ("exl", 8, U16), ("mk", 64, B), ("mkb", 64, B), ("DP", D, F), ("k8192", 64, B), ("k3072", 64, B),
-        ("se0", 128, B), ("se2", 128, B), ("se3", 128, B), ("se4n", 128, B), ("se0n", 128, B), ("se2n", 128, B),
-        ("sd", 128, B), ("sdn", 128, B), ("sb0", 128, B), ("sb1", 128, B), ("sb2", 128, B)):
+        ("At", C + 128, I32), ("Ot", C + 128, I32), ("Vt", C + 128, B), ("Yt", C, B), ("z0", D, B), ("z", S * D, B), ("zx", S * 16 * D, B),
+        ("mn0", 16 * D, B), ("mn1", 16 * D, B), ("gy0", 16 * D, B), ("gy1", 16 * D, B), ("vc", D, B), ("vcx", 16 * D, B),
+        ("hdi", 16, I32), ("hdo", 16, F), ("hl", 16 * S, U16), ("hT", 16 * S, F), ("hs", 16 * S, U16), ("hn", 16 * S, F), ("hK", 16, F),
+        ("ca", D, U16), ("co", D, U16), ("cah", D, H), ("coh", D, H), ("sc0", D, F), ("sc1", D, F), ("rn", 16, F), ("af", 16, F), ("bi", 16, I32), ("ki", 16, I32),
+        ("TM", D, H), ("TN", D, H), ("la", 16, U16), ("r2", 16, F), ("nver", 16, B), ("nz", 16, B), ("df", 16, F), ("dv", 16, F), ("rp", 8, F),
+        ("vz", 2304, H), ("oh", 1024, B), ("sq", 1280, F), ("rs16", 64, H), ("LS", D, F), ("gl", 16, U16),
+        ("K64", 64, F), ("prod", 64, H), ("E", 1280, B), ("KD", 128, F), ("NW", D, I32), ("vg", D, B), ("nv", 128, B),
+        ("PS", 128, F), ("XD", 16, F), ("of", 16, F), ("so", 16, U16), ("hob", 512, F),
+        ("ipi", 1, I32), ("p16i", 1, I32), ("pgi", 1, I32), ("p16", 1, F), ("pg", 1, F), ("kcode", 1, F), ("sv", 8, F), ("sxi", 2, I32), ("sx", 2, U16),
+        ("i128", 128, F), ("ub", 1, F), ("imod", 256, F), ("idiv", 128, F), ("itwo", 128, F), ("r32", 128, F), ("DUM", 16, F),
+        ("If", 128, F), ("Ib", 128, B), ("Inb", 128, B), ("U", 128, B), ("on", 128, B), ("m256", 256, F), ("bo", 128, F),
+        ("boh", 128, B), ("jj", 8, B), ("blk", 8, B), ("nblk", 8, B), ("rst", 128, F), ("brow", 128, B), ("cl", 256, B), ("cr", 128, B),
+        ("io64", 64, B), ("exl", 16, U16), ("bob", 128, B), ("mkL", 192, B), ("mkC", 128, B), ("mkR", 320, B),
+        ("se0", 128, B), ("se1", 128, B), ("se2", 128, B), ("se3", 128, B), ("se4n", 128, B), ("se2n", 128, B), ("sd", 128, B)):
     SCRATCH[_n] = ("sbuf", [128, _w], _d)
 for _i in range(8):
     SCRATCH["P%d" % _i] = ("psum", [128, 512], F)
-SEMAPHORES = ["cV", "cA", "cP", "cG"] + ["d%d" % i for i in range(24)] + ["az1", "az2", "az3", "ah1", "ah2", "ah3", "lz", "lh"]
+SEMAPHORES = (["cV", "cA", "cP", "cG"] + ["d%d" % i for i in range(32)] + ["a%s%d" % (k, i) for k in "zlt" for i in (1, 2, 3)] + ["lz", "ll", "lt"])
 
 
 def rank_program(g, core, T, topo):
@@ -35,81 +41,74 @@ def rank_program(g, core, T, topo):
     if rank is None:
         return
     Q = {"V": g.vector, "A": g.scalar, "P": g.tensor, "G": g, "S": g.sync}
-    cnt = {}
-    seen = {q: {} for q in Q}
-    snap = {}
+    calls = [None]
     Wr, Rd = {}, {}
-    toks = [None]
+    held, turn = {}, [0.0]
 
-    def new_token(q, sem, n):
-        cnt[sem] = cnt.get(sem, 0) + n
-        toks.append((sem, cnt[sem], q))
-        snap[len(toks) - 1] = dict(seen[q])
-        return len(toks) - 1
-
-    def wait_tok(q, i):
-        sem, v, _ = toks[i]
-        if seen[q].get(sem, 0) >= v:
-            return
-        Q[q].wait_ge(T.sem[sem], v)
-        seen[q][sem] = v
-        for s2, v2 in snap[i].items():
-            if v2 > seen[q].get(s2, 0):
-                seen[q][s2] = v2
-
-    def track(name):
-        if name not in Wr:
-            Wr[name] = np.zeros(SCRATCH[name][1][1], np.int64)
-            Rd[name] = {}
-
-    def need(q, reads, writes):
-        ids = set()
-        for kind, accs in ((0, reads), (1, writes)):
-            for name, cols in accs:
-                track(name)
-                if SCRATCH[name][0] == "psum":
-                    for arr in list(Rd[name].values()) + [Wr[name]]:
-                        ids.update(int(x) for x in np.unique(arr) if x and toks[int(x)][2] != q)
-                else:
-                    ids.update(int(x) for x in np.unique(Wr[name][cols]))
-                    if kind:
-                        for arr in Rd[name].values():
-                            ids.update(int(x) for x in np.unique(arr[cols]))
-        ids.discard(0)
-        if q == "P":
-            ids = {i for i in ids if toks[i][0] != "cP"}
-        for i in sorted(ids, reverse=True):
-            wait_tok(q, i)
-
-    def note(tok, reads, writes):
-        key = toks[tok][0]
-        for name, cols in reads:
-            Rd[name].setdefault(key, np.zeros(len(Wr[name]), np.int64))[cols] = tok
+    def record(q, issue, sem, n, hold, lat, reads, writes, after=(), free=False):
+        pre = set(after)
+        me = len(calls)
+        for name, cols in reads + writes:
+            if name not in Wr:
+                Wr[name] = np.zeros(SCRATCH[name][1][1], np.int64)
+                Rd[name] = []
+        banks = {nm for nm, _ in reads + writes if SCRATCH[nm][0] == "psum"}
+        for name in banks:
+            users = Rd[name]
+            if free:
+                pre.add(users[0])
+            elif q == "P" or any(calls[u][0] != q for u in users):
+                held[name], Rd[name] = users, []
+            pre.update(held.get(name, []))
+            Rd[name].append(me)
+        reads, writes = [x for x in reads if x[0] not in banks], [x for x in writes if x[0] not in banks]
+        for name, cols in reads + writes:
+            pre.update(set(Wr[name][cols].tolist()))
         for name, cols in writes:
-            Wr[name][cols] = tok
+            pre.update(r for r, m in Rd[name] if m[cols].any())
+            Wr[name][cols] = me
+            for r, m in Rd[name]:
+                m[cols] = False
+            Rd[name] = [x for x in Rd[name] if x[1].any()]
+        for name, cols in reads:
+            m = np.zeros(len(Wr[name]), bool)
+            m[cols] = True
+            Rd[name].append((me, m))
+        pre.discard(0)
+        pre.discard(me)
+        calls.append([q, issue, sem, n, hold, lat, pre, turn[0]])
+        return me
 
-    def op(q, call, writes, reads):
-        rr = [a for x in reads for a in x[1]]
-        ww = [a for x in writes for a in x[1]]
-        need(q, rr, ww)
-        call().then_inc(T.sem["c" + q], 1)
-        note(new_token(q, "c" + q, 1), rr, ww)
+    def at(x):
+        turn[0] = x
+
+    def op(q, call, writes, reads, cost, free=False):
+        record(q, lambda: call().then_inc(T.sem["c" + q], 1), "c" + q, 1, cost, cost,
+               [a for x in reads for a in x[1]], [a for x in writes for a in x[1]], free=free)
 
     def X(name, a=None, b=None, s=1, p=None):
         a = 0 if a is None else a
         b = SCRATCH[name][1][1] if b is None else b
         ps = slice(None) if p is None else slice(p[0], p[1])
         ap = T[name][ps, a:b] if s == 1 else T[name][ps, a:b:s]
-        return (ap, [(name, np.arange(a, b, s))])
+        return (ap, [(name, slice(a, b, s))], len(range(a, b, s)), SCRATCH[name][2] in (B, H, U16), SCRATCH[name][0] == "psum", False)
 
     def IND(win, off):
-        return (win[0].indirect(off[0]), win[1] + off[1])
+        return (win[0].indirect(off[0]), win[1] + off[1], 16 * off[2], False, False, True)
+
+    def vcost(o, i, rate):
+        if o[5] or i[5]:
+            return 0.06 + i[2] * (SCATTER if o[5] else GATHER) * CYC
+        return max(64, i[2] * rate) * CYC
 
     def cp(o, i):
-        op("V", lambda: g.vector.tensor_copy(o[0], i[0]), [o], [i])
+        if o[5]:
+            op("V", lambda: g.vector.tensor_copy(o[0], i[0]), [(0, o[1][:1])], [i, (0, o[1][1:])], vcost(o, i, 1))
+        else:
+            op("V", lambda: g.vector.tensor_copy(o[0], i[0]), [o], [i], vcost(o, i, 0.5 if o[3] and i[3] else 1))
 
     def tt(o, a, b, f):
-        op("V", lambda: g.vector.tensor_tensor(o[0], a[0], b[0], f), [o], [a, b])
+        op("V", lambda: g.vector.tensor_tensor(o[0], a[0], b[0], f), [o], [a, b], vcost(o, a, 1 if a[4] or b[4] else 2))
 
     def val(x, rs):
         if isinstance(x, tuple):
@@ -120,371 +119,400 @@ def rank_program(g, core, T, topo):
     def ts(o, a, s1, f1, s2=None, f2=None):
         rs = [a]
         v1, v2 = val(s1, rs), val(s2, rs)
+        cost = vcost(o, a, 0.5 if o[3] and a[3] else 1)
         if f2 is None:
-            op("V", lambda: g.vector.tensor_scalar(o[0], a[0], v1, None, f1), [o], rs)
+            op("V", lambda: g.vector.tensor_scalar(o[0], a[0], v1, None, f1), [o], rs, cost)
         else:
-            op("V", lambda: g.vector.tensor_scalar(o[0], a[0], v1, v2, f1, f2), [o], rs)
+            op("V", lambda: g.vector.tensor_scalar(o[0], a[0], v1, v2, f1, f2), [o], rs, cost)
 
-    def scan(o, d0, d1, f1):
-        op("V", lambda: g.vector.tensor_tensor_scan(o[0], d0[0], d1[0], 0.0, ALU.mult, f1), [o], [d0, d1])
+    def fill(o, c):
+        op("V", lambda: g.vector.memset(o[0], c), [o], [], vcost(o, o, 0.5 if o[3] else 1))
+
+    def scan(o, d0, d1):
+        op("V", lambda: g.vector.tensor_tensor_scan(o[0], d0[0], d1[0], 0.0, ALU.mult, ALU.max), [o], [d0, d1], vcost(o, d1, 1))
 
     def act(o, i, f=AF.Copy, bias=0.0, scale=1.0):
         rs = [i]
         b, c = val(bias, rs), val(scale, rs)
-        op("A", lambda: g.scalar.activation(o[0], i[0], f, bias=b, scale=c), [o], rs)
+        op("A", lambda: g.scalar.activation(o[0], i[0], f, bias=b, scale=c), [o], rs, vcost(o, i, 1))
 
     def mm(o, l, r, start, stop):
-        op("P", lambda: g.tensor.matmul(o[0], l[0], r[0], start, stop), [o], [l, r])
+        op("P", lambda: g.tensor.matmul(o[0], l[0], r[0], start, stop), [o], [l, r], max(min(64, l[2]), r[2]) * (1 if l[3] else 4) * PECYC,
+           not start and not stop)
 
     def iota(o, pat, base, cm):
+        cost = 0.14 + 2 * o[2] * CYC
         if SCRATCH[o[1][0][0]][2] == I32:
-            op("G", lambda: g.iota(o[0], pat, base, cm), [o], [])
+            op("G", lambda: g.iota(o[0], pat, base, cm), [o], [], cost)
         else:
-            op("G", lambda: g.iota(o[0], pat, base, cm, allow_small_or_imprecise_dtypes=True), [o], [])
+            op("G", lambda: g.iota(o[0], pat, base, cm, allow_small_or_imprecise_dtypes=True), [o], [], cost)
 
-    nd = [0]
+    def sel(o, i, pat, f, c, base, cm):
+        op("G", lambda: g.affine_select(o[0], i[0], pat, f, c, base, cm), [o], [i], 0.18 + 2 * o[2] * CYC)
 
-    def dma(q, o, i):
-        need(q, i[1], o[1])
+    nd, loaded = [0], [2.0]
+
+    def dma(q, o, i, nbytes=0):
         sem = "d%d" % nd[0]
         nd[0] += 1
-        Q[q].dma_start(o[0], i[0]).then_inc(T.sem[sem], 16)
-        note(new_token(q, sem, 16), i[1], o[1])
+        loaded[0] += nbytes / LOADRATE
+        record(q, lambda: Q[q].dma_start(o[0], i[0]).then_inc(T.sem[sem], 16), sem, 16, 0.05, loaded[0] if nbytes else 2.0, i[1], o[1])
 
-    def send(dst, name, a, b, name2, a2, rsem, lsem):
-        src = X(name, a, b)
-        need("G", src[1], [])
+    def send(hops, src, name, a, rsem, lsem):
+        dst, frm = T.cores[(rank + hops * HOP) % N], T.cores[(rank - hops * HOP) % N]
         rid, pid, _ = topo.addr(dst)
         eng = topo.engines(core, dst)[:8]
-        g.remote_dma(T[name2][:, a2:a2 + b - a], src[0], T.sem[rsem], T.sem[lsem], pid, rid, sum(1 << e for e in eng))
-        note(new_token("G", lsem, len(eng)), src[1], [])
-
-    def arrives(name, a, b, rsem, src):
-        track(name)
-        cnt[rsem] = len(topo.engines(src, core)[:8])
-        toks.append((rsem, cnt[rsem], "R"))
-        snap[len(toks) - 1] = {}
-        Wr[name][a:b] = len(toks) - 1
+        s = record("G", lambda: g.remote_dma(T[name][:, a:a + src[2]], src[0], T.sem[rsem], T.sem[lsem], pid, rid, sum(1 << e for e in eng)),
+                   lsem, len(eng), 0.3, HOPTIME, src[1], [])
+        record("R", None, rsem, len(topo.engines(frm, core)[:8]), 0.0, 0.0, [], X(name, a, a + src[2])[1], [s])
 
     EQ, MU, AD, SU = ALU.is_equal, ALU.mult, ALU.add, ALU.subtract
     dma("S", X("hdi"), (T.hd[:, :], []))
     dma("A", X("z0"), (T.zc[:, :], []))
     w = C // 4
     for i in range(4):
-        dma("SA"[i % 2], X("aoraw", i * w, i * w + w), (T.ao[:, i * w:i * w + w], []))
-    dma("S", X("VY", C, C + C // 2), (T.yd[:, 0:C // 2], []))
-    dma("A", X("VY", C + C // 2, PAD), (T.yd[:, C // 2:C], []))
-    dma("S", X("VY", 0, C // 2), (T.ve[:, 0:C // 2], []))
-    dma("A", X("VY", C // 2, C), (T.ve[:, C // 2:C], []))
+        dma("SA"[i % 2], X("Ot", i * w, i * w + w), (T.ao[:, i * w:i * w + w], []), 512 * w)
+    for i in range(4):
+        dma("SA"[i % 2], X("Yt", i * w, i * w + w), (T.yd[:, i * w:i * w + w], []), 256 * w)
+    for i in range(2):
+        dma("SA"[i], X("Vt", i * 2 * w, i * 2 * w + 2 * w), (T.ve[:, i * 2 * w:i * 2 * w + 2 * w], []), 512 * w)
+    act(X("z", 0, D), X("z0"), scale=-1.0)
+    for r in range(1, N):
+        send(r, X("z", 0, D), "z", r * D, "az%d" % r, "lz")
+    on = X("on")
     iota(X("ipi"), [[0, 1]], 0, 1)
-    iota(X("ip"), [[0, 1]], 0, 1)
     iota(X("i128"), [[1, 128]], 0, 0)
     iota(X("imod"), [[0, 16], [1, 16]], 0, 0)
     iota(X("idiv"), [[1, 8], [0, 16]], 0, 0)
-    iota(X("on"), [[0, 128]], 1, 0)
-    iota(X("ipad"), [[1, 256]], PAD, 0)
-    iota(X("io64"), [[1, 64]], 1, 0)
-    iota(X("mk", 16, 64), [[0, 48]], 0, 0)
-    iota(X("mkb", 16, 64), [[0, 48]], 4608, 0)
-    iota(X("k8192"), [[0, 64]], 8192, 0)
-    iota(X("k3072"), [[0, 64]], 3072, 0)
-    for r in range(1, N):
-        send(T.cores[(rank + r * HOP) % N], "z0", 0, D, "zin", (r - 1) * D, "az%d" % r, "lz")
-        arrives("zin", (r - 1) * D, r * D, "az%d" % r, T.cores[(rank - r * HOP) % N])
-        arrives("hin", (r - 1) * 32, r * 32, "ah%d" % r, T.cores[(rank - HOP) % N])
-    p, p16, pg = X("ip"), X("p16"), X("pg")
+    iota(X("itwo"), [[0, 4], [1, 16], [0, 2]], 0, 0)
+    iota(X("r32"), [[0, 4], [1, 32]], 0, 0)
+    iota(X("DUM"), [[0, 2], [16, 8]], C, 0)
+    iota(X("io64"), [[1, 64]], 1 - 256, 0)
+    fill(on, 1.0)
+    fill(X("vz"), 0.0)
+    fill(X("vz", 4, 2165, 144), 1.0)
+    sel(X("Ib"), on, [[-1, 128]], EQ, 0.0, 0, 1)
+    p16, pg = X("p16"), X("pg")
     ts(X("p16i"), X("ipi"), 15, ALU.bitwise_and)
     ts(X("pgi"), X("ipi"), 4, ALU.logical_shift_right)
-    ts(X("If"), X("i128"), p, EQ)
-    cp(X("p16"), X("p16i"))
-    cp(X("pg"), X("pgi"))
-    ts(X("vz", 0, 256), X("imod"), 0.0, MU)
-    cp(X("vz", 256, 512), X("vz", 0, 256))
-    cp(X("vz", 512, 1024), X("vz", 0, 512))
-    cp(X("vz", 1024, 2048), X("vz", 0, 1024))
-    cp(X("vz", 2048, 2304), X("vz", 0, 256))
-    ts(X("vz", 4, 2165, 144), X("imod", 0, 16), 0.0, MU, 1.0, AD)
-    cp(X("hl0"), X("hdi"))
+    ts(X("sxi", 0, 1), X("ipi"), 3, ALU.bitwise_and)
+    ts(X("ub"), X("ipi"), -200.0, MU, 100.0, AD)
+    cp(p16, X("p16i"))
+    cp(pg, X("pgi"))
+    ts(X("sx", 0, 1), X("sxi", 0, 1), 32.0, MU, 31.0, AD)
+    cp(X("hl", 0, 16), X("hdi"))
     ts(X("hdo"), X("hdi"), -1536.0, AD)
     ts(X("jj"), X("i128", 0, 8), pg, EQ)
     ts(X("bo"), X("idiv"), pg, EQ)
-    cp(X("exl"), X("i128", 0, 8))
+    cp(X("exl"), X("i128", 0, 16))
     ts(X("m256"), X("imod"), p16, EQ)
+    ts(X("DUM"), X("DUM"), p16, AD)
     sv = lambda i: X("sv", i, i + 1)
     for v in range(4):
         ts(sv(v), p16, float(v), EQ)
-    for i, c in ((4, -8192.0), (5, 1536.0), (6, 4608.0)):
-        ts(sv(i), p16, 4.0, EQ, c, MU)
-    tt(sv(8), sv(0), sv(5), AD)
-    tt(sv(9), sv(1), sv(5), AD)
-    tt(sv(10), sv(2), sv(6), AD)
-    tt(sv(11), sv(1), sv(0), SU)
-    ts(X("mk", 0, 16), X("imod", 0, 16), p16, ALU.is_le, 16384.0, MU)
-    act(X("Ib"), X("If"))
-    act(X("Inb"), X("If"), scale=-1.0)
-    act(X("brow"), X("imod", 0, 128), bias=61440.0, scale=-4096.0)
-    act(X("rst"), X("imod"), AF.Sign)
-    act(X("ub"), p, bias=100.0, scale=-200.0)
+    ts(sv(4), p16, 4.0, EQ, -8192.0, MU)
     act(X("U"), X("i128"), AF.Sigmoid, X("ub"), 200.0)
-    for k in range(16):
-        act(X("z16a", k, 16 * D, 16), X("z0"))
-    act(X("blk"), X("jj"), scale=65536.0)
-    act(X("nblk"), X("jj"), scale=-65536.0)
+    sel(X("U"), X("U"), [[1, 128]], ALU.not_equal, -255.0, 0, -1)
+    act(X("If"), X("Ib"))
+    act(X("Inb"), X("Ib"), scale=-1.0)
+    act(X("brow"), X("imod", 0, 128), bias=61440.0, scale=-4096.0)
+    act(X("rst"), X("imod", 0, 128), AF.Sign)
+    act(X("r32"), X("r32"), AF.Sign)
+    for nm, c in (("blk", 65536.0), ("nblk", -65536.0)):
+        act(X(nm), X("jj"), scale=c)
     bo = X("bo")
-    act(X("zblk"), bo, scale=65536.0)
     act(X("boh"), bo, scale=8192.0)
     act(X("kcode"), p16, bias=15.0, scale=-1.0)
-    act(X("mkb", 0, 16), X("mk", 0, 16), bias=4608.0)
-    for nm, v in (("se0", 0), ("se2", 2), ("se3", 3), ("se4n", 4), ("sb0", 8), ("sb1", 9), ("sb2", 10), ("sd", 11)):
+    for nm, v in (("se0", 0), ("se1", 1), ("se2", 2), ("se3", 3), ("se4n", 4)):
         act(X(nm), bo, scale=sv(v))
-    for nm, src in (("se0n", "se0"), ("se2n", "se2"), ("sdn", "sd")):
-        act(X(nm), X(src), scale=-1.0)
-    blocks = []
-    o = 0
-    for q in range(4):
-        blocks.append((o, 64 - 16 * q))
-        o += 2 * (64 - 16 * q)
+    act(X("se2n"), X("se2"), scale=-1.0)
+    tt(X("sd"), X("se1"), X("se0"), SU)
+    act(X("sd"), X("sd"), scale=4096.0)
+    act(X("bob"), bo)
+    act(X("mkL"), X("m256", 0, 192), bias=-16384.0, scale=16384.0 + 1536.0)
+    for hh in range(2):
+        act(X("mkC", hh, 128, 2), X("m256", 0, 64), bias=-2.0 ** 22, scale=2.0 ** 22 + 8192.0 * (1 - hh))
+    blocks = [(0, 64), (128, 48), (224, 32), (288, 16)]
+    fill(X("mkR"), 1536.0)
+    ts(X("mkR", 0, 32), X("itwo", 0, 32), p16, ALU.is_le, 16384.0, MU)
+    act(X("mkR", 0, 32), X("mkR", 0, 32), bias=1536.0)
+    for o, wd in blocks[1:]:
+        act(X("mkR", o, o + 32), X("mkR", 0, 32))
+    two = (0, 2)
+    sel(X("cr", p=two), X("brow", p=two), [[0, 128]], EQ, 240.0 * 65536, 0, 1)
+    for hf in range(2):
+        sel(X("cl", 128 * hf, 128 * hf + 128, 1, two), X("on", p=two), [[-1, 128]], ALU.is_ge, 0.0, NA[0][hf] + 999, -1000)
     for i in range(4):
-        ts(X("AO", i * w, i * w + w), X("aoraw", i * w, i * w + w), 4095, ALU.bitwise_and)
+        ts(X("At", i * w, i * w + w), X("Ot", i * w, i * w + w), 4095, ALU.bitwise_and)
+        ts(X("At", i * w, i * w + w), X("At", i * w, i * w + w), -1536.0, AD)
+    for i in range(4):
+        ts(X("Yt", i * w, i * w + w), X("Yt", i * w, i * w + w), -1.0, MU)
+    At, Ot, Vt, Yt = X("At", 0, C), X("Ot", 0, C), X("Vt", 0, C), X("Yt")
 
-    half = lambda nm, hf: X(nm, 8 * hf, 8 * hf + 8)
+    half = lambda nm, hf, t=0: X(nm, 16 * t + 8 * hf, 16 * t + 8 * hf + 8)
 
-    def conv_a(nm, hf):
-        tt(X("TM", 128 * hf, 128 * hf + 128), IND(half(nm, hf), X("exl")), X("m256", 128 * hf, 128 * hf + 128), MU)
+    def conv(src, tm, hf, out):
+        tt(X(tm, 128 * hf, 128 * hf + 128), IND(src, X("exl", 0, 8)), X("m256", 0, 128), MU)
+        mm(out, X(tm, 128 * hf, 128 * hf + 128), X("jj"), True, True)
 
-    def conv_b(out, hf):
-        mm(out, X("TM", 128 * hf, 128 * hf + 128), X("jj"), True, True)
+    def spread(how, dst, src, a, b, ks):
+        for k in ks:
+            o, i = X(dst, 16 * a + k, 16 * b, 16), X(src, a, b)
+            if how == "G":
+                sel(o, i, [[0, b - a]], ALU.is_ge, 0.0, 0, 0)
+            else:
+                (act if how == "A" else cp)(o, i)
 
-    lists = lambda hf: X("P2" if hf == 0 else "P3", 384, 392)
+    nb = [0]
 
-    def embed():
-        for hf in range(2):
-            mm(X("P%d" % hf, 0, 128), X("cah", 128 * hf, 128 * hf + 128), X("Ib"), True, False)
-
-    def reduce(d0, d1, w):
-        hf, b = d0 // 128, d0 % 128
-        for k in range(16):
-            mm(X("P%d" % hf, k, 128, 16, (b, b + d1 - d0)), X("mn", 16 * d0 + k, 16 * d1, 16), X(w), False, False)
-
-    def close(hf):
-        mm(X("P%d" % hf, 0, 128), X("on", p=(0, 1)), X("brow", p=(0, 1)), False, True)
-
-    def best_of(hf):
-        scan(X("sc", 128 * hf, 128 * hf + 128), X("rst", 0, 128), X("P%d" % hf, 0, 128), ALU.max)
-
-    best = X("sc", 15, 256, 16)
-    bst = lambda hf: X("sc", 128 * hf + 15, 128 * hf + 128, 16)
-    for t in range(S):
-        last = t == S - 1
-        hl = X("hl0") if t == 0 else X("hin", (t - 1) * 32, (t - 1) * 32 + 16)
-        zrow = X("z0", V1, D) if t == 0 else X("zin", (t - 1) * D + V1, t * D)
-        z16 = ("z16a", "z16b")[t % 2]
-        if not last:
+    def stage(t0, st, hf, win, lst, lsth, other, f, func, bias, scale, wt):
+        bank, mn, gy, mo = "P%d" % hf, "mn%d" % st, "gy%d" % st, 128 * hf
+        wide = lambda nm, a, b: X(nm, 16 * a, 16 * b)
+        oth = lambda a, b: X(other[0], other[1] + 16 * a, other[1] + 16 * b)
+        at(t0)
+        mm(X(bank, 0, 128), X(lsth, mo, mo + 128), X("Ib"), True, False)
+        v0 = mo + NA[st][hf]
+        for a in range(mo, v0, 32):
+            b = min(v0, a + 32)
+            pb = X("P%d" % (4 + nb[0] % 4), 0, 16 * (b - a))
+            nb[0] += 1
+            act(wide(gy, a, b), IND(win, X(lst, a, b)))
+            mm(pb, X("Inb"), oth(a, b), True, False)
+            mm(pb, X("Ib"), wide(gy, a, b), False, True)
+            act(wide(mn, a, b), pb, func, bias, scale)
+        for a in range(v0, mo + 128, VCHUNK):
+            b = min(mo + 128, a + VCHUNK)
+            tt(wide(mn, a, b), IND(win, X(lst, a, b)), oth(a, b), f)
+        for d0, d1 in zip(CUTS[st][hf], CUTS[st][hf][1:]):
             for k in range(16):
-                zo, zi = X(("z16a", "z16b")[(t + 1) % 2], k, 16 * D, 16), X("zin", t * D, t * D + D)
-                op("G", lambda: g.affine_select(zo[0], zi[0], [[0, D]], ALU.is_ge, 0.0, 0, 0), [zo], [zi])
-        for i, d0 in enumerate(range(V1, D, 32)):
-            mm(X("P%d" % (3 + i)), X("Ib"), X(z16, 16 * d0, 16 * d0 + 512), True, False)
-        cp(X("ca"), IND(X("AO", 0, C), hl))
-        ts(X("cah"), X("ca"), -1536.0, AD)
-        embed()
-        mm(X("P1", 0, 128, 1, (64, 128)), zrow, X("zblk"), False, False)
+                mm(X(bank, k, 128, 16, (d0, d1)), X(mn, 16 * (mo + d0) + k, 16 * (mo + d1), 16), X(wt), False, False)
+        rows = (0, 2 - st)
+        mm(X(bank, 0, 128), X("cl", mo, mo + 128, 1, rows), X("cr", p=rows), False, True)
+        scan(X("sc%d" % st, mo, mo + 128), X("rst"), X(bank, 0, 128))
+        return X("sc%d" % st, mo + 15, mo + 128, 16)
 
-        def vmin(a, b):
-            tt(X("mn", 16 * a, 16 * b), IND(X("VY", C, PAD), X("ca", a, b)), X(z16, 16 * a, 16 * b), ALU.min)
-        if t == 0:
-            for i in range(4):
-                ts(X("AO", C + i * w, C + i * w + w), X("aoraw", i * w, i * w + w), 12, ALU.logical_shift_right)
-        vmin(0, 128)
-        for i, d0 in enumerate(range(V1, D, 32)):
-            act(X("gy", 512 * i, 512 * i + 512), IND(X("VY", C, PAD), X("ca", d0, d0 + 32)))
-            mm(X("P%d" % (3 + i)), X("Inb"), X("gy", 512 * i, 512 * i + 512), False, True)
-        for i, d0 in enumerate(range(V1, D, 32)):
-            act(X("mn", 16 * d0, 16 * d0 + 512), X("P%d" % (3 + i)), AF.Relu)
-        act(X("vc"), IND(X("VY", 0, C), hl))
-        for j in range(16):
-            act(X("vcx", j, 16 * D, 16), X("vc"))
-        reduce(V1, V1 + 32, "nblk")
-        reduce(0, 128, "blk")
-        close(0)
-        vmin(128, 160)
-        reduce(128, 160, "blk")
-        vmin(160, V1)
-        reduce(V1 + 32, D, "nblk")
-        reduce(160, V1, "blk")
-        close(1)
-        if t == 0:
-            for hf in range(2):
-                conv_a("hdo", hf)
-                conv_b(lists(hf), hf)
-                cp(half("hT", hf), lists(hf))
-        else:
-            ts(X("hT"), X("hin", (t - 1) * 32 + 16, t * 32), -1536.0, AD)
-        cp(X("vz", 0, 2161, 144), X("hT"))
-        best_of(0)
-        ts(half("rn", 0), bst(0), MAGIC, AD, MAGIC, SU)
-        tt(half("af", 0), bst(0), half("rn", 0), SU)
-        best_of(1)
-        conv_a("af", 0)
-        ts(half("rn", 1), bst(1), MAGIC, AD, MAGIC, SU)
-        conv_b(lists(0), 0)
-        cp(X("vz", 2, 1011, 144), half("af", 0))
-        tt(half("af", 1), bst(1), half("rn", 1), SU)
-        ts(half("la", 0), lists(0), 1536.0, AD)
-        conv_a("af", 1)
-        conv_b(lists(1), 1)
-        cp(X("ca", 0, 128), IND(X("AO", C, PAD), half("la", 0)))
-        ts(half("la", 1), lists(1), 1536.0, AD)
-        cp(X("vz", 1154, 2163, 144), half("af", 1))
-        cp(X("ca", 128, 256), IND(X("AO", C, PAD), half("la", 1)))
+    spread("A", "zx", "z", 0, D, range(16))
+    for hf in range(2):
+        conv(half("hdo", hf), "TN", hf, X("P2", 8 * hf, 8 * hf + 8))
+    cp(X("hT", 0, 16), X("P2", 0, 16))
+    for t in range(1, S):
+        at(100 * (t - 1) + TURN["zx"])
+        spread("G", "zx", "z", D * t, D * t + D, range(GZ))
+        spread("A", "zx", "z", D * t, D * t + D, range(GZ, 16))
+    for t in range(S):
+        last, t0 = t == S - 1, 100 * t
+        hT = X("hT", 16 * t, 16 * t + 16)
+        for hf in range(2):
+            at(t0 + TURN["ca"][hf])
+            for a, b in ((0, 2), (2, 8)) if hf == 0 and CASPLIT else ((8 * hf, 8 * hf + 8),):
+                ts(X("ca", 16 * a, 16 * b), IND(At, X("hl", 16 * t + a, 16 * t + b)), 1536.0, AD)
+            at(t0 + TURN["s1"][hf])
+            ts(X("cah", 128 * hf, 128 * hf + 128), X("ca", 128 * hf, 128 * hf + 128), -1536.0, AD)
+        at(t0 + TURN["vg"])
+        act(X("vc"), IND(Vt, X("hl", 16 * t, 16 * t + 16)))
+        for hf in range(2):
+            at(t0 + TURN["vc"][hf])
+            spread("G", "vcx", "vc", 128 * hf, 128 * hf + 128, range(GVC[hf]))
+            spread("V", "vcx", "vc", 128 * hf, 128 * hf + 128, range(GVC[hf], 16))
+        at(t0 + TURN["k"])
+        cp(X("vz", 0, 2161, 144), hT)
+        ts(X("hK"), hT, 61440.0, AD)
+        for hf in range(2):
+            best = stage(t0 + TURN["s1"][hf], 0, hf, Yt, "ca", "cah", ("zx", 16 * D * t), ALU.max, AF.Relu, 0.0, 1.0, "nblk")
+            at(t0 + TURN["d1"][hf])
+            ts(half("rn", hf), best, MAGIC, AD, MAGIC, SU)
+            tt(half("af", hf), best, half("rn", hf), SU)
+            conv(half("af", hf), "TM", hf, X("P2", 8 * hf, 8 * hf + 8))
+            ts(half("la", hf), X("P2", 8 * hf, 8 * hf + 8), 1536.0, AD)
+            ts(X("co", 128 * hf, 128 * hf + 128), IND(Ot, half("la", hf)), 1.0 / 4096, MU, -0.375, AD)
+            ts(X("coh", 128 * hf, 128 * hf + 128), X("co", 128 * hf, 128 * hf + 128), -1536.0, AD)
+        at(t0 + TURN["k"])
+        cp(X("vz", 2, 2163, 144), X("af"))
         ts(X("bi"), X("rn"), 1.0 / 4096, MU)
-        for i, d0 in enumerate(range(V2, D, 32)):
-            mm(X("P%d" % (5 + i)), X("Inb"), X("vcx", 16 * d0, 16 * d0 + 512), True, False)
-
-        def vgt(a, b):
-            tt(X("mn", 16 * a, 16 * b), IND(X("VY", 0, C), X("ca", a, b)), X("vcx", 16 * a, 16 * b), ALU.is_gt)
-        ts(X("cah"), X("ca"), -1536.0, AD)
-        vgt(0, 128)
-        for i, d0 in enumerate(range(V2, D, 32)):
-            act(X("gy", 512 * i, 512 * i + 512), IND(X("VY", 0, C), X("ca", d0, d0 + 32)))
-            mm(X("P%d" % (5 + i)), X("Ib"), X("gy", 512 * i, 512 * i + 512), False, True)
-        for i, d0 in enumerate(range(V2, D, 32)):
-            act(X("mn", 16 * d0, 16 * d0 + 512), X("P%d" % (5 + i)), AF.Sigmoid, -100.0, 200.0)
         ts(X("ki"), X("bi"), 15, ALU.bitwise_and)
-        vgt(128, V2)
         cp(X("vz", 3, 2164, 144), X("ki"))
-        embed()
-        reduce(0, 128, "blk")
-        close(0)
-        reduce(128, 256, "blk")
-        close(1)
-        if t == 0:
-            tt(X("DP"), X("m256"), X("ipad"), MU)
-        best_of(0)
-        best_of(1)
-        ts(X("rn"), best, MAGIC, AD, MAGIC, SU)
-        ts(X("ver"), best, 12.0 * 65536 - 1536, ALU.is_ge)
-        tt(X("af"), best, X("rn"), SU)
-        tt(X("nz"), X("af"), X("hT"), ALU.not_equal)
-        tt(X("df"), X("af"), X("hT"), SU)
-        tt(X("prop"), X("nz"), X("ver"), ALU.is_gt)
-        cp(X("vz", 1, 2162, 144), X("af"))
-        mm(X("P2", 144, 152), X("U"), X("prop", 0, 8), True, True)
-        mm(X("P2", 152, 160), X("U"), X("prop", 8, 16), True, False)
-        mm(X("P2", 152, 160), X("on"), X("prop", 0, 8), False, True)
-        tt(X("rp"), X("P2", 144, 160), X("prop"), MU)
-        for i in range(VOH, 16):
-            act(X("sq", 64 * (i - VOH), 64 * (i - VOH) + 64), X("io64"), AF.Square, X("rp", i, i + 1), -1.0)
-        for i in range(VOH, 16):
-            act(X("oh", 64 * i, 64 * i + 64), X("sq", 64 * (i - VOH), 64 * (i - VOH) + 64), AF.Relu, 1.0, -1.0)
-        for i in range(16):
-            if i < VOH:
-                ts(X("oh", 64 * i, 64 * i + 64), X("io64"), X("rp", i, i + 1), EQ)
-            hf, gg = i // 8, i % 8
-            mm(X("P2", 0, 64), X("vz", 128 * gg + 1152 * hf, 128 * gg + 1152 * hf + 128), X("oh", 64 * i, 64 * i + 64), i == 0, i == 15)
-        tt(X("df"), X("df"), X("ver"), MU)
-        cp(X("rs16"), X("P2", 0, 64))
-        tt(X("hn"), X("df"), X("hT"), AD)
-        for v, nm in enumerate(("sb0", "sb1", "sb2", "se3")):
-            mm(X("P3", 64 * v, 64 * v + 64), X(nm), X("rs16"), True, True)
-        mm(X("P2", 64, 128), X("Ib"), X("k3072"), True, False)
-
-        def rows(bank, q, hh, nm, src, m):
-            o, wd = blocks[q]
-            mm(X(bank, o + hh * wd, o + hh * wd + wd), X("Ib"), X(m, 0, wd), True, False)
-            mm(X(bank, o + hh * wd, o + hh * wd + wd), X(nm), X(src, 16 * q, 64), False, True)
-        for q in range(4):
-            rows("P4", q, 0, "sb0", "rs16", "mk")
-            rows("P4", q, 1, "sb1", "rs16", "mk")
-        tt(X("LM", 0, 192), X("P3", 0, 192), X("m256", 0, 192), MU)
-        ts(X("K64"), X("P3", 192, 256), X("kcode"), EQ)
-        scan(X("LS", 0, 192), X("rst", 0, 192), X("LM", 0, 192), AD)
-        cp(X("gl", 0, 12), X("LS", 15, 192, 16))
-        tt(X("prod"), IND(X("AO", 0, C), X("gl", 4, 8)), X("K64"), MU)
-        mm(X("P2", 64, 128), bo, X("prod"), False, True)
-        for q in range(4):
-            rows("P5", q, 0, "sb2", "rs16", "mk")
+        for hf in range(2):
+            best = stage(t0 + TURN["s2"][hf], 1, hf, Vt, "co", "coh", ("vcx", 0), ALU.is_gt, AF.Sigmoid, -100.0, 200.0, "blk")
+            at(t0 + TURN["d2"][hf])
+            h = lambda nm: half(nm, hf)
+            tt(h("nz"), best, h("hK"), ALU.not_equal)
+            ts(h("nver"), best, 12.0 * 65536 - 1536, ALU.is_ge, -1.0, MU)
+            ts(h("r2"), best, MAGIC, AD, MAGIC, SU)
+            tt(X("vz", 1 + 1152 * hf, 1011 + 1152 * hf, 144), best, h("r2"), SU)
+            na = AOH if hf else 0
+            terms = [(on, half("nz", 0)), (on, half("nver", 0))][:2 * hf] + [(X("U"), h("nz")), (X("U"), h("nver"))]
+            for bank in ("P2", "P0")[:2 if na else 1]:
+                for i, (l, r) in enumerate(terms):
+                    mm(X(bank, 16, 24), l, r, i == 0, i == len(terms) - 1)
+            if na:
+                act(X("rp"), X("P0", 16, 24))
+            for gg in range(8 - na, 8):
+                act(X("sq", 64 * gg, 64 * gg + 64), X("io64"), AF.Square, X("rp", gg, gg + 1), -1.0)
+            for gg in range(8):
+                i = 8 * hf + gg
+                if gg < 8 - na:
+                    ts(X("oh", 64 * i, 64 * i + 64), X("io64"), X("P2", 16 + gg, 17 + gg), EQ)
+                else:
+                    act(X("oh", 64 * i, 64 * i + 64), X("sq", 64 * gg, 64 * gg + 64), AF.Relu, 1.0, -1.0)
+                mm(X("P3", 0, 64), X("vz", 128 * gg + 1152 * hf, 128 * gg + 1152 * hf + 128), X("oh", 64 * i, 64 * i + 64), i == 0, i == 15)
+        hn = X("hn", 16 * t, 16 * t + 16)
+        at(t0 + TURN["hn"])
+        tt(X("df"), X("vz", 1, 2162, 144), hT, SU)
+        tt(X("dv"), X("df"), X("nver"), MU)
+        tt(hn, hT, X("dv"), SU)
         if not last:
-            conv_a("hn", 0)
-            conv_a("hn", 1)
-            ts(X("hsend", 32 * t + 16, 32 * t + 32), X("hn"), 1536.0, AD)
-        ts(X("rb16"), X("P2", 64, 128), -4608.0, AD)
-        tt(X("LM", 192, 256), X("P2", 64, 128), X("m256", 0, 64), MU)
-        scan(X("LS", 192, 256), X("rst", 0, 64), X("LM", 192, 256), AD)
-        cp(X("gl", 12, 16), X("LS", 207, 256, 16))
-        for q in range(4):
-            rows("P5", q, 1, "se0", "rb16", "mkb")
-        if not last:
+            tt(X("TN"), IND(hn, X("exl")), X("m256"), MU)
             for hf in range(2):
-                conv_b(X("P2", 128 + 8 * hf, 136 + 8 * hf), hf)
-            ts(X("hsend", 32 * t, 32 * t + 16), X("P2", 128, 144), 1536.0, AD)
-            send(T.cores[(rank + HOP) % N], "hsend", 32 * t, 32 * t + 32, "hin", 32 * t, "ah%d" % (t + 1), "lh")
-            mm(X("P6", 0, 64), X("se0"), X("rb16"), True, False)
-            mm(X("P6", 0, 64), X("se2n"), X("rs16"), False, True)
-            mm(X("P6", 64, 128), X("se0n"), X("rb16"), True, False)
-            mm(X("P6", 64, 128), X("se2"), X("rs16"), False, True)
-            mm(X("P6", 128, 192), X("sd"), X("rs16"), True, True)
-            mm(X("P6", 192, 256), X("sdn"), X("rs16"), True, True)
-        mm(X("P7", 0, 64), X("Ib"), X("k8192"), True, False)
-        mm(X("P7", 0, 64), X("se4n"), X("rs16"), False, False)
-        pr = {}
-        e = 0
-        for bank, base in (("P4", 0), ("P5", 128)):
-            for q in range(4):
-                o, wd = blocks[q]
-                for v in range(2):
-                    ls = base + 64 * v + 16 * q + 15
-                    pr[bank, q, v] = (X(bank, o, o + 2 * wd), X("LS", ls, ls + 1), e, wd)
-                    e += 2 * wd
-
-        def count(key, fin=False):
-            _, _, e, wd = pr[key]
+                mm(X("P2", 32 + 8 * hf, 40 + 8 * hf), X("TN", 128 * hf, 128 * hf + 128), X("jj"), True, True)
+            ts(X("hs", 16 * t, 16 * t + 16), X("P2", 32, 48), 1536.0, AD)
+            send(1, X("hs", 16 * t, 16 * t + 16), "hl", 16 * t + 16, "al%d" % (t + 1), "ll")
+            send(1, hn, "hT", 16 * t + 16, "at%d" % (t + 1), "lt")
+        at(t0 + TURN["ho"])
+        mm(X("P2", 160, 288, 1, (0, 16)), hn, X("If"), True, True)
+        act(X("hob", 128 * t, 128 * t + 128, 1, (0, 16)), X("P2", 160, 288, 1, (0, 16)), AF.Copy, 1536.0)
+        for hf in range(2):
+            c0 = t * D + hf * 128
+            dma("S", (T.ho[:, c0:c0 + 128], []), X("hob", 128 * t, 128 * t + 128, 1, (8 * hf, 8 * hf + 8)))
+        at(t0 + TURN["x"])
+        cp(X("rs16"), X("P3", 0, 64))
+        mm(X("P6", 0, 192), X("Ib"), X("mkL", 0, 192), True, False)
+        for v in (1, 0, 2):
+            mm(X("P6", 64 * v, 64 * v + 64), X("se%d" % v), X("rs16"), False, v == 2)
+        mm(X("P1", 128, 192), X("se3"), X("rs16"), True, True)
+        scan(X("LS", 64, 128), X("rst", 0, 64), X("P6", 64, 128))
+        cp(X("gl", 4, 8), X("LS", 79, 128, 16))
+        ts(X("K64"), X("P1", 128, 192), X("kcode"), EQ)
+        tt(X("prod"), IND(At, X("gl", 4, 8)), X("K64"), MU)
+        for v in (0, 2):
+            scan(X("LS", 64 * v, 64 * v + 64), X("rst", 0, 64), X("P6", 64 * v, 64 * v + 64))
+        cp(X("gl", 0, 4), X("LS", 15, 64, 16))
+        mm(X("P0", 64, 128), X("Ib"), X("mkL", 0, 64), True, False)
+        mm(X("P0", 64, 128), X("bob"), X("prod"), False, True)
+        scan(X("LS", 192, 256), X("rst", 0, 64), X("P0", 64, 128))
+        cp(X("gl", 8, 16), X("LS", 143, 256, 16))
+        for bank, srcs in (("P4", (("se0", "rs16"), ("se1", "rs16"))), ("P5", (("se2", "rs16"), ("bob", "prod")))):
+            mm(X(bank, 0, 320), X("Ib"), X("mkR"), True, False)
             for hh in range(2):
-                mm(X("P7", 64 - wd, 64), X("boh"), X("E", e + hh * wd, e + hh * wd + wd), False, fin and hh == 1)
-
-        def by_scalar(keys):
-            for key in keys:
-                src, col, e, wd = pr[key]
-                act(X("sq", e, e + 2 * wd), src, AF.Square, col, -1.0)
-            for key in keys:
-                src, col, e, wd = pr[key]
-                act(X("E", e, e + 2 * wd), X("sq", e, e + 2 * wd), AF.Relu, 1.0, -1.0)
-                count(key)
-
-        def by_vector(key):
-            src, col, e, wd = pr[key]
+                for q, (o, wd) in enumerate(blocks):
+                    mm(X(bank, o + hh, o + 2 * wd, 2), X(srcs[hh][0]), X(srcs[hh][1], 16 * q, 64), False, hh == 1 and q == 3)
+        mm(X("P7", 0, 128), X("Ib"), X("mkC"), True, False)
+        e, pairs = 0, []
+        for bank, base in (("P4", 0), ("P5", 128)):
+            for q, (o, wd) in enumerate(blocks):
+                for v in range(2):
+                    pairs.append((X(bank, o, o + 2 * wd), X("LS", base + 64 * v + 16 * q + 15, base + 64 * v + 16 * q + 16), e, wd))
+                    e += 2 * wd
+        for src, col, e, wd in pairs[APAIR:8] + pairs[8 + BPAIR:]:
             ts(X("E", e, e + 2 * wd), src, col, EQ)
-        by_scalar([("P4", q, v) for q in range(4) for v in range(2)])
-        by_scalar([("P5", q, v) for q in (2, 3) for v in range(2)])
-        act(X("vg"), IND(X("VY", 0, PAD), X("gl")))
-        for q in (1, 0):
-            for v in range(2):
-                by_vector(("P5", q, v))
-                count(("P5", q, v), q == 0 and v == 1)
-        for o, ya, yb in ((0, "Inb", "Ib"), (64, "Ib", "Inb")):
+        for part in (pairs[:APAIR], pairs[8:8 + BPAIR]):
+            for src, col, e, wd in part:
+                act(X("sq", e, e + 2 * wd), src, AF.Square, col, -1.0)
+            e0, e1 = (part[0][2], part[-1][2] + 2 * part[-1][3]) if part else (0, 0)
+            for e in range(e0, e1, RELU):
+                act(X("E", e, min(e1, e + RELU)), X("sq", e, min(e1, e + RELU)), AF.Relu, 1.0, -1.0)
+        for src, col, e, wd in pairs:
+            mm(X("P7", 128 - 2 * wd, 128), X("boh"), X("E", e, e + 2 * wd), False, False)
+        mm(X("P7", 0, 128, 2), X("se4n"), X("rs16"), False, True)
+        at(t0 + TURN["nw"])
+        act(X("vg", 0, 128), IND(Vt, X("gl", 0, 8)))
+        act(X("vg", 128, 256), IND(Yt, X("gl", 8, 16)))
+        for o, ya, yb in ((0, "Ib", "Inb"), (64, "Inb", "Ib")):
             mm(X("P3", 256 + o, 320 + o), X("Ib"), X("vg", o, o + 64), True, False)
             mm(X("P3", 256 + o, 320 + o), X(ya), X("vg", 128, 192), False, False)
             mm(X("P3", 256 + o, 320 + o), X(yb), X("vg", 192, 256), False, True)
         act(X("nv"), X("P3", 256, 384))
-        mm(X("P2", 160, 288, 1, (0, 16)), X("hn"), X("If"), True, True)
-        act(X("hob", 128 * t, 128 * t + 128, 1, (0, 16)), X("P2", 160, 288, 1, (0, 16)), AF.Copy, 1536.0)
         if not last:
+            mm(X("P1", 256, 320), X("bob"), X("prod"), True, False)
+            mm(X("P1", 256, 320), X("se2n"), X("rs16"), False, True)
+            mm(X("P1", 320, 384), X("sd"), X("rs16"), True, True)
+            for v in range(2):
+                tt(X("KD", 64 * v, 64 * v + 64), X("P1", 256 + 64 * v, 320 + 64 * v), X("K64"), MU)
             for v in range(4):
-                tt(X("KD", 64 * v, 64 * v + 64), X("P6", 64 * v, 64 * v + 64), X("K64"), MU)
-            tt(X("NW"), IND(X("AO", 0, PAD), X("gl")), X("KD"), AD)
-        nq = 2 if last else 4
-        for v in range(nq):
-            tt(X("PM", 64 * v, 64 * v + 64), X("P7", 0, 64), X("DP", 64 * v, 64 * v + 64), ALU.min)
-        scan(X("PS", 0, 64 * nq), X("rst", 0, 64 * nq), X("PM", 0, 64 * nq), AD)
-        tt(X("of", 0, 4 * nq), X("PS", 15, 64 * nq, 16), X("LS", 15, 64 * nq, 16), ALU.max)
-        cp(X("so", 0, 4 * nq), X("of", 0, 4 * nq))
+                at(t0 + TURN["upd" if v // 2 else "nw"])
+                tt(X("NW", 64 * v, 64 * v + 64), IND((At, Ot)[v // 2], X("gl", 4 * v, 4 * v + 4)), X("KD", 64 * (v // 2), 64 * (v // 2) + 64), (AD, SU)[v % 2])
+        at(t0 + TURN["x"])
+        scan(X("PS"), X("r32"), X("P7", 0, 128))
+        tt(X("XD"), IND(X("PS"), X("sx", 0, 1)), X("DUM"), ALU.min)
+        tt(X("of"), X("XD"), X("LS", 15, 256, 16), ALU.max)
+        cp(X("so"), X("of"))
         if not last:
-            cp(IND(X("AO"), X("so")), X("NW"))
-        cp(IND(X("VY"), X("so", 0, 8)), X("nv"))
-        for hf in range(2):
-            c0 = t * D + hf * 128
-            dma("S", (T.ho[:, c0:c0 + 128], []), X("hob", 128 * t, 128 * t + 128, 1, (8 * hf, 8 * hf + 8)))
-    dma("S", (T.vo[:, :], []), X("VY", 0, C))
+            cp(IND(X("At"), X("so", 0, 8)), X("NW", 0, 128))
+        at(t0 + TURN["vt"])
+        cp(IND(X("Vt"), X("so", 0, 8)), X("nv"))
+        at(t0 + TURN["upd"])
+        if not last:
+            cp(IND(X("Ot"), X("so", 8, 16)), X("NW", 128, 256))
+    dma("S", (T.vo[:, :], []), Vt)
+
+    n = len(calls)
+    delay = lambda a, b: 0.0 if calls[a][0] == calls[b][0] == "P" or calls[b][0] == "R" else WAKE
+    after, left = [[] for _ in range(n)], [0] * n
+    for i in range(n - 1, 0, -1):
+        left[i] = len(calls[i][6])
+        for p in calls[i][6]:
+            after[p].append(i)
+            calls[p][7] = min(calls[p][7], calls[i][7])
+    start, ready, idle, order = [0.0] * n, [0.0] * n, {q: 0.0 for q in "VAPGSR"}, []
+    cand = {q: [i for i in range(1, n) if calls[i][0] == q and not left[i]] for q in idle}
+    while len(order) < n - 1:
+        t0, q = min((max(idle[q], min(ready[i] for i in cand[q])), q) for q in cand if cand[q])
+        i = min((calls[i][7], i) for i in cand[q] if ready[i] <= t0 + (AHEAD if q in "VA" else PAHEAD))[1]
+        if ready[i] > t0:
+            i = min([(calls[j][7], j) for j in cand[q] if ready[j] <= t0 and t0 + calls[j][4] <= ready[i] + SLACK] or [(0, i)])[1]
+        cand[q].remove(i)
+        order.append(i)
+        start[i] = max(t0, ready[i])
+        idle[q] = start[i] + calls[i][4]
+        for j in after[i]:
+            ready[j] = max(ready[j], start[i] + calls[i][5] + delay(i, j))
+            left[j] -= 1
+            if not left[j]:
+                cand[calls[j][0]].append(j)
+
+    def justify(order, before, gap):
+        at_, busy = [0.0] * n, {q: [] for q in idle}
+        for i in order:
+            t, slots, hold = max([at_[p] + gap(p, i) for p in before[i]] + [0.0]), busy[calls[i][0]], calls[i][4]
+            k = len(slots)
+            while k and slots[k - 1][1] > t:
+                k -= 1
+            while k < len(slots) and t + hold > slots[k][0] + 1e-9:
+                t = max(t, slots[k][1])
+                k += 1
+            slots.insert(k, (t, t + hold))
+            at_[i] = t
+        return at_
+    pre = [[]] + [c[6] for c in calls[1:]]
+    span = lambda s: max(s[i] + calls[i][5] for i in range(1, n))
+    cur = start
+    for _ in range(ROUNDS):
+        back = justify(sorted(range(1, n), key=lambda i: (-cur[i] - calls[i][4], -i)), after,
+                       lambda p, i: calls[p][4] + calls[i][5] - calls[i][4] + delay(i, p))
+        cur = justify(sorted(range(1, n), key=lambda i: (-back[i] - calls[i][4], i)), pre, lambda p, i: calls[p][5] + delay(p, i))
+        if span(cur) < span(start):
+            start = cur
+    order = sorted(range(1, n), key=lambda i: (start[i] if calls[i][6] or calls[i][3] != 16 else -1.0, i))
+    cnt, tok, seen, snap = {}, {}, {q: {} for q in Q}, {}
+    for i in order:
+        if calls[i][0] == "R":
+            tok[i], snap[i] = (calls[i][2], calls[i][3]), {}
+            cnt[calls[i][2]] = calls[i][3]
+    for i in order:
+        q, issue, sem, inc = calls[i][:4]
+        if q == "R":
+            continue
+        for p in sorted(calls[i][6], key=lambda p: -start[p]):
+            if q == "P" and calls[p][0] == "P":
+                continue
+            s, v = tok[p]
+            if seen[q].get(s, 0) < v:
+                Q[q].wait_ge(T.sem[s], v)
+                seen[q][s] = v
+                for s2, v2 in snap[p].items():
+                    seen[q][s2] = max(seen[q].get(s2, 0), v2)
+        issue()
+        cnt[sem] = cnt.get(sem, 0) + inc
+        tok[i], snap[i] = (sem, cnt[sem]), dict(seen[q])
     for sem, v in sorted(cnt.items()):
         if seen["G"].get(sem, 0) < v:
             g.wait_ge(T.sem[sem], v)

@@ -2,38 +2,48 @@ import numpy as np
 from concourse.mybir import AluOpType as ALU, ActivationFunctionType as AF
 
 N, C, D, S, HOP = 4, 3072, 256, 4, 1
-NA = ((48, 80), (80, 48))
+NA = ((48, 72), (80, 40))
 CUTS = (((0, 128), (0, 128)), ((0, 128), (0, 128)))
-VCHUNK = 32
-CASPLIT = 1
+ACHUNK = 32
+VCHUNK = 16
+CASPLIT, R2MERGE, KA = 0, 0, 0
+AOCUT, YCUT = (0, 1024, 2048, C), (0, C)
+FIX, XWAKE = 0.01, -0.03
+HSPLIT, GCP, MARGIN, LATE = 0, 0, 0.0, 3.0
+JITTER, JFRAC, SEED = 0.0, 0.1, 0
+DONE, TNA = 0.3, 0
+COVER, VERA, NPASS, PEFIX = 0, 1, 6, 0.0
+AMUL, AVC, AOH0 = 0.95, 0, 2
+AFIX, KV, GMUL, RCALL = 0.025, 1, 1.05, 0.9
+STR, VSPLIT, Z0 = (0, 0), 1, "A"
 AOH = 0
-APAIR, BPAIR, RELU = 6, 0, 256
-GZ, GVC = 16, (10, 8)
-TURN = dict(ca=(0, 1), s1=(4, 5), d1=(6, 9), s2=(12, 14), d2=(12, 17), vg=9, vc=(10, 13), vt=102, upd=107, k=15, hn=26, ho=68, x=25, nw=26, zx=73)
-AHEAD, PAHEAD, SLACK, ROUNDS = 0.1, 0.0, 0.02, 2
+APAIR, BPAIR, RELU = 8, 0, 256
+GZ, GVC = (8, 10), (10, 8)
+TURN = dict(ca=(0, 1), s1=(5, 5), d1=(5, 9), s2=(16, 9), d2=(12, 17), vg=3, vc=(3, 11), vt=108, upd=106, k=18, hn=(11, 16), ho=93, x=25, nw=24, zx=40, z1=30, at=24)
+AHEAD, PAHEAD, SLACK, ROUNDS = 0.1, 0.2, 0.05, 3
 MAGIC = 1.5 * 2.0 ** 35
-CYC, PECYC, WAKE, GATHER, SCATTER, HOPTIME, LOADRATE = 0.9e-3, 0.65e-3, 0.13, 1.56, 3.8, 2.5, 250e3
+CYC, PECYC, WAKE, GATHER, SCATTER, HOPTIME, LOADRATE = 0.86e-3, 0.65e-3, 0.21, 1.35, 3.6, 4.0, 500e3
 F, B, H, I32, U16 = "float32", "bfloat16", "float16", "int32", "uint16"
 SCRATCH = {}
 for _n, _w, _d in (
-        ("At", C + 128, I32), ("Ot", C + 128, I32), ("Vt", C + 128, B), ("Yt", C, B), ("z0", D, B), ("z", S * D, B), ("zx", S * 16 * D, B),
+        ("At", C + 128, F), ("Ai", C, I32), ("ag", 128, F), ("bon", 128, B), ("Ot", C + 128, I32), ("Vt", C + 128, B), ("Yt", C, B), ("z0", D, B), ("z", S * D, B), ("zx", S * 16 * D, B),
         ("mn0", 16 * D, B), ("mn1", 16 * D, B), ("gy0", 16 * D, B), ("gy1", 16 * D, B), ("vc", D, B), ("vcx", 16 * D, B),
         ("hdi", 16, I32), ("hdo", 16, F), ("hl", 16 * S, U16), ("hT", 16 * S, F), ("hs", 16 * S, U16), ("hn", 16 * S, F), ("hK", 16, F),
-        ("ca", D, U16), ("co", D, U16), ("cah", D, H), ("coh", D, H), ("sc0", D, F), ("sc1", D, F), ("rn", 16, F), ("af", 16, F), ("bi", 16, I32), ("ki", 16, I32),
-        ("TM", D, H), ("TN", D, H), ("la", 16, U16), ("r2", 16, F), ("nver", 16, B), ("nz", 16, B), ("df", 16, F), ("dv", 16, F), ("rp", 8, F),
+        ("ca", D, U16), ("co", D, U16), ("cah", D, H), ("coh", D, H), ("sc0", D, F), ("sc1", 272, F), ("rn", 16, F), ("af", 16, F), ("k1", 16, F), ("k2", 16, F),
+        ("TM", D, H), ("TN", D, H), ("TF", D, F), ("jf", 8, F), ("kq", 64, F), ("la", 16, U16), ("r2", 16, F), ("nver", 16, B), ("nz", 16, B), ("r3", 16, F), ("I17", 136, B), ("b17", 136, B), ("r17", 136, F), ("i17", 136, F), ("rp", 16, F),
         ("vz", 2304, H), ("oh", 1024, B), ("sq", 1280, F), ("rs16", 64, H), ("LS", D, F), ("gl", 16, U16),
-        ("K64", 64, F), ("prod", 64, H), ("E", 1280, B), ("KD", 128, F), ("NW", D, I32), ("vg", D, B), ("nv", 128, B),
+        ("K64", 64, F), ("prod", 64, H), ("E", 1280, B), ("KD", 192, F), ("NW", D, I32), ("vg", D, B), ("nv", 128, B),
         ("PS", 128, F), ("XD", 16, F), ("of", 16, F), ("so", 16, U16), ("hob", 512, F),
         ("ipi", 1, I32), ("p16i", 1, I32), ("pgi", 1, I32), ("p16", 1, F), ("pg", 1, F), ("kcode", 1, F), ("sv", 8, F), ("sxi", 2, I32), ("sx", 2, U16),
-        ("i128", 128, F), ("ub", 1, F), ("imod", 256, F), ("idiv", 128, F), ("itwo", 128, F), ("r32", 128, F), ("DUM", 16, F),
-        ("If", 128, F), ("Ib", 128, B), ("Inb", 128, B), ("U", 128, B), ("on", 128, B), ("m256", 256, F), ("bo", 128, F),
+        ("i128", 128, F), ("ub", 1, F), ("imod", 256, F), ("idiv", 128, B), ("itwo", 128, F), ("r32", 128, F), ("DUM", 16, F),
+        ("If", 128, F), ("Ib", 128, B), ("Inb", 128, B), ("U", 128, B), ("Un", 128, B), ("non", 128, B), ("on", 128, B), ("m256", 256, F), ("bo", 128, F),
         ("boh", 128, B), ("jj", 8, B), ("blk", 8, B), ("nblk", 8, B), ("rst", 128, F), ("brow", 128, B), ("cl", 256, B), ("cr", 128, B),
         ("io64", 64, B), ("exl", 16, U16), ("bob", 128, B), ("mkL", 192, B), ("mkC", 128, B), ("mkR", 320, B),
         ("se0", 128, B), ("se1", 128, B), ("se2", 128, B), ("se3", 128, B), ("se4n", 128, B), ("se2n", 128, B), ("sd", 128, B)):
     SCRATCH[_n] = ("sbuf", [128, _w], _d)
 for _i in range(8):
     SCRATCH["P%d" % _i] = ("psum", [128, 512], F)
-SEMAPHORES = (["cV", "cA", "cP", "cG"] + ["d%d" % i for i in range(32)] + ["a%s%d" % (k, i) for k in "zlt" for i in (1, 2, 3)] + ["lz", "ll", "lt"])
+SEMAPHORES = (["cV", "cA", "cP", "cG"] + ["d%d" % i for i in range(32)] + ["a%s%d" % (k, i) for k in "zt" for i in (1, 2, 3)] + ["al%d" % i for i in range(6)] + ["lz", "ll", "lt"])
 
 
 def rank_program(g, core, T, topo):
@@ -43,11 +53,13 @@ def rank_program(g, core, T, topo):
     Q = {"V": g.vector, "A": g.scalar, "P": g.tensor, "G": g, "S": g.sync}
     calls = [None]
     Wr, Rd = {}, {}
-    held, turn = {}, [0.0]
+    held, turn, raw = {}, [0.0], {}
+    nth, kinds, kind = {}, {}, [0]
 
     def record(q, issue, sem, n, hold, lat, reads, writes, after=(), free=False):
         pre = set(after)
         me = len(calls)
+        names = [x[0] for x in writes + reads] or [""]
         for name, cols in reads + writes:
             if name not in Wr:
                 Wr[name] = np.zeros(SCRATCH[name][1][1], np.int64)
@@ -62,9 +74,12 @@ def rank_program(g, core, T, topo):
             pre.update(held.get(name, []))
             Rd[name].append(me)
         reads, writes = [x for x in reads if x[0] not in banks], [x for x in writes if x[0] not in banks]
-        for name, cols in reads + writes:
-            pre.update(set(Wr[name][cols].tolist()))
+        raw[me] = set()
+        for name, cols in reads:
+            raw[me].update(Wr[name][cols].tolist())
+        pre.update(raw[me])
         for name, cols in writes:
+            pre.update(set(Wr[name][cols].tolist()))
             pre.update(r for r, m in Rd[name] if m[cols].any())
             Wr[name][cols] = me
             for r, m in Rd[name]:
@@ -76,6 +91,9 @@ def rank_program(g, core, T, topo):
             Rd[name].append((me, m))
         pre.discard(0)
         pre.discard(me)
+        key = (q, names[0], names[-1])
+        nth[key] = nth.get(key, 0) + 1
+        kind.append(kinds.setdefault(key + (nth[key],), len(kinds)))
         calls.append([q, issue, sem, n, hold, lat, pre, turn[0]])
         return me
 
@@ -98,8 +116,8 @@ def rank_program(g, core, T, topo):
 
     def vcost(o, i, rate):
         if o[5] or i[5]:
-            return 0.06 + i[2] * (SCATTER if o[5] else GATHER) * CYC
-        return max(64, i[2] * rate) * CYC
+            return FIX + 0.06 + i[2] * (SCATTER if o[5] else GATHER) * CYC
+        return FIX + max(64, i[2] * rate) * CYC
 
     def cp(o, i):
         if o[5]:
@@ -108,7 +126,7 @@ def rank_program(g, core, T, topo):
             op("V", lambda: g.vector.tensor_copy(o[0], i[0]), [o], [i], vcost(o, i, 0.5 if o[3] and i[3] else 1))
 
     def tt(o, a, b, f):
-        op("V", lambda: g.vector.tensor_tensor(o[0], a[0], b[0], f), [o], [a, b], vcost(o, a, 1 if a[4] or b[4] else 2))
+        op("V", lambda: g.vector.tensor_tensor(o[0], a[0], b[0], f), [(0, o[1][:1])], [a, b, (0, o[1][1:])], vcost(o, a, 1 if a[4] or b[4] else 2))
 
     def val(x, rs):
         if isinstance(x, tuple):
@@ -134,11 +152,19 @@ def rank_program(g, core, T, topo):
     def act(o, i, f=AF.Copy, bias=0.0, scale=1.0):
         rs = [i]
         b, c = val(bias, rs), val(scale, rs)
-        op("A", lambda: g.scalar.activation(o[0], i[0], f, bias=b, scale=c), [o], rs, vcost(o, i, 1))
+        op("A", lambda: g.scalar.activation(o[0], i[0], f, bias=b, scale=c), [o], rs, vcost(o, i, 1) * AMUL + AFIX)
 
-    def mm(o, l, r, start, stop):
-        op("P", lambda: g.tensor.matmul(o[0], l[0], r[0], start, stop), [o], [l, r], max(min(64, l[2]), r[2]) * (1 if l[3] else 4) * PECYC,
-           not start and not stop)
+    groups, closes = [], set()
+
+    def mm(o, l, r, start, stop=None, chain=False):
+        me = len(calls)
+        if start:
+            groups.append([])
+            opened[o[1][0][0]] = groups[-1]
+        opened[o[1][0][0]].append(me)
+        op("P", lambda: g.tensor.matmul(o[0], l[0], r[0], start, me in closes), [o], [l, r],
+           max(min(64, l[2]), r[2]) * (1 if l[3] else 4) * PECYC + PEFIX, not start and not chain)
+    opened = {}
 
     def iota(o, pat, base, cm):
         cost = 0.14 + 2 * o[2] * CYC
@@ -148,7 +174,13 @@ def rank_program(g, core, T, topo):
             op("G", lambda: g.iota(o[0], pat, base, cm, allow_small_or_imprecise_dtypes=True), [o], [], cost)
 
     def sel(o, i, pat, f, c, base, cm):
-        op("G", lambda: g.affine_select(o[0], i[0], pat, f, c, base, cm), [o], [i], 0.18 + 2 * o[2] * CYC)
+        op("G", lambda: g.affine_select(o[0], i[0], pat, f, c, base, cm), [o], [i], (0.18 + 2 * o[2] * CYC) * GMUL)
+
+    def gcp(o, i):
+        if GCP:
+            sel(o, i, [[0, o[2]]], ALU.is_ge, 0.0, 0, 0)
+        else:
+            cp(o, i)
 
     nd, loaded = [0], [2.0]
 
@@ -158,24 +190,25 @@ def rank_program(g, core, T, topo):
         loaded[0] += nbytes / LOADRATE
         record(q, lambda: Q[q].dma_start(o[0], i[0]).then_inc(T.sem[sem], 16), sem, 16, 0.05, loaded[0] if nbytes else 2.0, i[1], o[1])
 
-    def send(hops, src, name, a, rsem, lsem):
+    def send(hops, src, name, a, rsem, lsem, behind=()):
         dst, frm = T.cores[(rank + hops * HOP) % N], T.cores[(rank - hops * HOP) % N]
         rid, pid, _ = topo.addr(dst)
         eng = topo.engines(core, dst)[:8]
         s = record("G", lambda: g.remote_dma(T[name][:, a:a + src[2]], src[0], T.sem[rsem], T.sem[lsem], pid, rid, sum(1 << e for e in eng)),
-                   lsem, len(eng), 0.3, HOPTIME, src[1], [])
-        record("R", None, rsem, len(topo.engines(frm, core)[:8]), 0.0, 0.0, [], X(name, a, a + src[2])[1], [s])
+                   lsem, len(eng), RCALL, HOPTIME, src[1], [], behind)
+        loose.update((p, s) for p in behind)
+        record("R", None, rsem, len(topo.engines(frm, core)[:8]), 0.0, LATE if name != "hl" else 0.0, [], X(name, a, a + src[2])[1], [s])
+        return s
+    loose = set()
 
     EQ, MU, AD, SU = ALU.is_equal, ALU.mult, ALU.add, ALU.subtract
     dma("S", X("hdi"), (T.hd[:, :], []))
     dma("A", X("z0"), (T.zc[:, :], []))
-    w = C // 4
-    for i in range(4):
-        dma("SA"[i % 2], X("Ot", i * w, i * w + w), (T.ao[:, i * w:i * w + w], []), 512 * w)
-    for i in range(4):
-        dma("SA"[i % 2], X("Yt", i * w, i * w + w), (T.yd[:, i * w:i * w + w], []), 256 * w)
-    for i in range(2):
-        dma("SA"[i], X("Vt", i * 2 * w, i * 2 * w + 2 * w), (T.ve[:, i * 2 * w:i * 2 * w + 2 * w], []), 512 * w)
+    i = 0
+    for nm, src, size, cuts in (("Ot", T.ao, 512, AOCUT), ("Yt", T.yd, 256, YCUT), ("Vt", T.ve, 256, (0, C))):
+        for a, b in zip(cuts, cuts[1:]):
+            dma("S", X(nm, a, b), (src[:, a:b], []), size * (b - a))
+            i += 1
     act(X("z", 0, D), X("z0"), scale=-1.0)
     for r in range(1, N):
         send(r, X("z", 0, D), "z", r * D, "az%d" % r, "lz")
@@ -203,32 +236,36 @@ def rank_program(g, core, T, topo):
     cp(X("hl", 0, 16), X("hdi"))
     ts(X("hdo"), X("hdi"), -1536.0, AD)
     ts(X("jj"), X("i128", 0, 8), pg, EQ)
-    ts(X("bo"), X("idiv"), pg, EQ)
     cp(X("exl"), X("i128", 0, 16))
     ts(X("m256"), X("imod"), p16, EQ)
     ts(X("DUM"), X("DUM"), p16, AD)
-    sv = lambda i: X("sv", i, i + 1)
-    for v in range(4):
-        ts(sv(v), p16, float(v), EQ)
-    ts(sv(4), p16, 4.0, EQ, -8192.0, MU)
     act(X("U"), X("i128"), AF.Sigmoid, X("ub"), 200.0)
     sel(X("U"), X("U"), [[1, 128]], ALU.not_equal, -255.0, 0, -1)
+    act(X("Un"), X("U"), scale=-1.0)
+    act(X("non"), on, scale=-1.0)
     act(X("If"), X("Ib"))
     act(X("Inb"), X("Ib"), scale=-1.0)
     act(X("brow"), X("imod", 0, 128), bias=61440.0, scale=-4096.0)
     act(X("rst"), X("imod", 0, 128), AF.Sign)
     act(X("r32"), X("r32"), AF.Sign)
-    for nm, c in (("blk", 65536.0), ("nblk", -65536.0)):
+    iota(X("i17"), [[0, 8], [1, 17]], 0, 0)
+    act(X("r17"), X("i17"), AF.Sign)
+    act(X("b17"), X("i17"), bias=61440.0, scale=-4096.0)
+    fill(X("b17", 16, 136, 17), 11.75 * 131072)
+    fill(X("I17"), 1.0)
+    sel(X("I17"), X("I17"), [[-16, 8], [-1, 17]], EQ, 0.0, 0, 1)
+    fill(X("I17", 16, 136, 17), 0.0)
+    for nm, c in (("blk", 131072.0), ("nblk", -65536.0), ("jf", 1.0)):
         act(X(nm), X("jj"), scale=c)
-    bo = X("bo")
-    act(X("boh"), bo, scale=8192.0)
-    act(X("kcode"), p16, bias=15.0, scale=-1.0)
-    for nm, v in (("se0", 0), ("se1", 1), ("se2", 2), ("se3", 3), ("se4n", 4)):
-        act(X(nm), bo, scale=sv(v))
-    act(X("se2n"), X("se2"), scale=-1.0)
-    tt(X("sd"), X("se1"), X("se0"), SU)
-    act(X("sd"), X("sd"), scale=4096.0)
-    act(X("bob"), bo)
+    act(X("kcode"), p16, bias=7.5, scale=-1.0)
+    row = [[-16, 8], [0, 16]]
+    for nm, v, c in (("se0", 0, 1.0), ("se1", 1, 1.0), ("se2", 2, 1.0), ("se3", 3, 1.0), ("se4n", 4, -8192.0), ("se2n", 2, -1.0), ("sd", 1, 4096.0)):
+        if c != 1.0:
+            fill(X(nm), c)
+        sel(X(nm), X(nm) if c != 1.0 else on, row, EQ, 0.0, -v, 1)
+    sel(X("sd"), X("sd"), row, ALU.not_equal, -4096.0, 0, 1)
+    for nm, c in (("bob", 1.0), ("boh", 8192.0), ("bon", -1.0)):
+        ts(X(nm), X("idiv"), pg, EQ, c, MU)
     act(X("mkL"), X("m256", 0, 192), bias=-16384.0, scale=16384.0 + 1536.0)
     for hh in range(2):
         act(X("mkC", hh, 128, 2), X("m256", 0, 64), bias=-2.0 ** 22, scale=2.0 ** 22 + 8192.0 * (1 - hh))
@@ -240,13 +277,18 @@ def rank_program(g, core, T, topo):
         act(X("mkR", o, o + 32), X("mkR", 0, 32))
     two = (0, 2)
     sel(X("cr", p=two), X("brow", p=two), [[0, 128]], EQ, 240.0 * 65536, 0, 1)
-    for hf in range(2):
-        sel(X("cl", 128 * hf, 128 * hf + 128, 1, two), X("on", p=two), [[-1, 128]], ALU.is_ge, 0.0, NA[0][hf] + 999, -1000)
-    for i in range(4):
-        ts(X("At", i * w, i * w + w), X("Ot", i * w, i * w + w), 4095, ALU.bitwise_and)
-        ts(X("At", i * w, i * w + w), X("At", i * w, i * w + w), -1536.0, AD)
-    for i in range(4):
-        ts(X("Yt", i * w, i * w + w), X("Yt", i * w, i * w + w), -1.0, MU)
+    sel(X("cl", 0, 128, 1, two), X("on", p=two), [[-1, 128]], ALU.is_ge, 0.0, NA[0][0] + 999, -1000)
+    sel(X("cl", 128, 256, 1, two), X("on", p=two), [[1, 128]], ALU.is_ge, 0.0, NA[0][1] + 872, -1000)
+    for a, b in zip(YCUT, YCUT[1:]):
+        m = a + (b - a) * 2 // 3
+        ts(X("Yt", a, m), X("Yt", a, m), -1.0, MU)
+        act(X("Yt", m, b), X("Yt", m, b), scale=-1.0)
+    at(TURN["at"])
+    w = C // NPASS
+    for a in range(0, C, w):
+        ts(X("Ai", a, a + w), X("Ot", a, a + w), 4095, ALU.bitwise_and)
+        ts(X("At", a, a + w), X("Ai", a, a + w), -1536.0, AD)
+    at(0)
     At, Ot, Vt, Yt = X("At", 0, C), X("Ot", 0, C), X("Vt", 0, C), X("Yt")
 
     half = lambda nm, hf, t=0: X(nm, 16 * t + 8 * hf, 16 * t + 8 * hf + 8)
@@ -270,55 +312,85 @@ def rank_program(g, core, T, topo):
         wide = lambda nm, a, b: X(nm, 16 * a, 16 * b)
         oth = lambda a, b: X(other[0], other[1] + 16 * a, other[1] + 16 * b)
         at(t0)
-        mm(X(bank, 0, 128), X(lsth, mo, mo + 128), X("Ib"), True, False)
-        v0 = mo + NA[st][hf]
-        for a in range(mo, v0, 32):
+        W = 16 + st
+        mm(X(bank, 0, 8 * W), X(lsth, mo, mo + 128), X(("Ib", "I17")[st]), True, False)
+        if st:
+            mm(X(bank, 16, 8 * W, W), X("Ib"), X("vz", 1152 * hf, 1010 + 1152 * hf, 144), False, False)
+        a0, v0 = (mo, mo + NA[st][0]) if hf == 0 else (D - NA[st][1], D)
+        got = 0
+        for a in range(a0, v0, 32):
             b = min(v0, a + 32)
             pb = X("P%d" % (4 + nb[0] % 4), 0, 16 * (b - a))
             nb[0] += 1
-            act(wide(gy, a, b), IND(win, X(lst, a, b)))
-            mm(pb, X("Inb"), oth(a, b), True, False)
-            mm(pb, X("Ib"), wide(gy, a, b), False, True)
+            if a >= got:
+                got = v0 if v0 - a <= ACHUNK else b
+                act(wide(gy, a, got), IND(win, X(lst, a, got)))
+            s0, s1 = SPREAD[st]
+            if s0 <= a and b <= s1:
+                mm(pb, X("Inb"), oth(a, b), True)
+                mm(pb, X("Ib"), wide(gy, a, b), False)
+            else:
+                if COVER:
+                    mm(pb, X("Ib"), wide(gy, a, b), True)
+                for k in range(16):
+                    mm(X(pb[1][0][0], k, 16 * (b - a), 16), X("Inb"), X(other[2], other[3] + a, other[3] + b), k == 0 and not COVER, chain=True)
+                if not COVER:
+                    mm(pb, X("Ib"), wide(gy, a, b), False, chain=True)
             act(wide(mn, a, b), pb, func, bias, scale)
-        for a in range(v0, mo + 128, VCHUNK):
-            b = min(mo + 128, a + VCHUNK)
+        v0, v1 = (v0, mo + 128) if hf == 0 else (mo, a0)
+        for a in range(v0, v1, VCHUNK):
+            b = min(v1, a + VCHUNK)
             tt(wide(mn, a, b), IND(win, X(lst, a, b)), oth(a, b), f)
         for d0, d1 in zip(CUTS[st][hf], CUTS[st][hf][1:]):
             for k in range(16):
-                mm(X(bank, k, 128, 16, (d0, d1)), X(mn, 16 * (mo + d0) + k, 16 * (mo + d1), 16), X(wt), False, False)
+                mm(X(bank, k, 8 * W, W, (d0, d1)), X(mn, 16 * (mo + d0) + k, 16 * (mo + d1), 16), X(wt), False, False)
         rows = (0, 2 - st)
-        mm(X(bank, 0, 128), X("cl", mo, mo + 128, 1, rows), X("cr", p=rows), False, True)
-        scan(X("sc%d" % st, mo, mo + 128), X("rst"), X(bank, 0, 128))
-        return X("sc%d" % st, mo + 15, mo + 128, 16)
+        mm(X(bank, 0, 8 * W), X("cl", mo, mo + 128, 1, rows), X(("cr", "b17")[st], p=rows), False, chain=len(CUTS[st][hf]) > 2)
+        scan(X("sc%d" % st, 8 * W * hf, 8 * W * (hf + 1)), X(("rst", "r17")[st]), X(bank, 0, 8 * W))
+        return X("sc%d" % st, 8 * W * hf + 15, 8 * W * (hf + 1), W)
 
-    spread("A", "zx", "z", 0, D, range(16))
+    SPREAD = [(NA[st][0] * (STR[st] > 0), D - NA[st][1] * (STR[st] > 1)) for st in range(2)]
+    spread(Z0, "zx", "z", SPREAD[0][0], SPREAD[0][1], range(16))
     for hf in range(2):
         conv(half("hdo", hf), "TN", hf, X("P2", 8 * hf, 8 * hf + 8))
     cp(X("hT", 0, 16), X("P2", 0, 16))
-    for t in range(1, S):
-        at(100 * (t - 1) + TURN["zx"])
-        spread("G", "zx", "z", D * t, D * t + D, range(GZ))
-        spread("A", "zx", "z", D * t, D * t + D, range(GZ, 16))
+
+    def costs(t, behind=()):
+        at(100 * (t - 2) + TURN["zx"] if t > 1 else TURN["z1"])
+        first = len(calls)
+        spread("G", "zx", "z", D * t + SPREAD[0][0], D * t + SPREAD[0][1], range(GZ[t > 1]))
+        for i in range(first, len(calls)):
+            calls[i][6].update(behind)
+            loose.update((p, i) for p in behind)
+        spread("A", "zx", "z", D * t + SPREAD[0][0], D * t + SPREAD[0][1], range(GZ[t > 1], 16))
+    costs(1)
     for t in range(S):
         last, t0 = t == S - 1, 100 * t
+        nth.clear()
         hT = X("hT", 16 * t, 16 * t + 16)
         for hf in range(2):
             at(t0 + TURN["ca"][hf])
             for a, b in ((0, 2), (2, 8)) if hf == 0 and CASPLIT else ((8 * hf, 8 * hf + 8),):
-                ts(X("ca", 16 * a, 16 * b), IND(At, X("hl", 16 * t + a, 16 * t + b)), 1536.0, AD)
+                if t:
+                    ts(X("ca", 16 * a, 16 * b), IND(At, X("hl", 16 * t + a, 16 * t + b)), 1536.0, AD)
+                else:
+                    ts(X("NW", 16 * a, 16 * b), IND(Ot, X("hl", a, b)), 4095, ALU.bitwise_and)
+                    cp(X("ca", 16 * a, 16 * b), X("NW", 16 * a, 16 * b))
             at(t0 + TURN["s1"][hf])
             ts(X("cah", 128 * hf, 128 * hf + 128), X("ca", 128 * hf, 128 * hf + 128), -1536.0, AD)
         at(t0 + TURN["vg"])
         act(X("vc"), IND(Vt, X("hl", 16 * t, 16 * t + 16)))
-        for hf in range(2):
+        s0, s1 = SPREAD[1]
+        for hf, (a, b) in enumerate(((s0, 128), (128, s1)) if VSPLIT else ((s0, s1),)):
             at(t0 + TURN["vc"][hf])
-            spread("G", "vcx", "vc", 128 * hf, 128 * hf + 128, range(GVC[hf]))
-            spread("V", "vcx", "vc", 128 * hf, 128 * hf + 128, range(GVC[hf], 16))
+            spread("G", "vcx", "vc", a, b, range(GVC[hf]))
+            spread("A", "vcx", "vc", a, b, range(GVC[hf], GVC[hf] + AVC))
+            spread("V", "vcx", "vc", a, b, range(GVC[hf] + AVC, 16))
         at(t0 + TURN["k"])
-        cp(X("vz", 0, 2161, 144), hT)
-        ts(X("hK"), hT, 61440.0, AD)
+        gcp(X("vz", 0, 2161, 144), hT)
+        act(X("hK"), hT, bias=61440.0)
         for hf in range(2):
-            best = stage(t0 + TURN["s1"][hf], 0, hf, Yt, "ca", "cah", ("zx", 16 * D * t), ALU.max, AF.Relu, 0.0, 1.0, "nblk")
+            best = stage(t0 + TURN["s1"][hf], 0, hf, Yt, "ca", "cah", ("zx", 16 * D * t, "z", D * t), ALU.max, AF.Relu, 0.0, 1.0, "nblk")
             at(t0 + TURN["d1"][hf])
             ts(half("rn", hf), best, MAGIC, AD, MAGIC, SU)
             tt(half("af", hf), best, half("rn", hf), SU)
@@ -327,46 +399,70 @@ def rank_program(g, core, T, topo):
             ts(X("co", 128 * hf, 128 * hf + 128), IND(Ot, half("la", hf)), 1.0 / 4096, MU, -0.375, AD)
             ts(X("coh", 128 * hf, 128 * hf + 128), X("co", 128 * hf, 128 * hf + 128), -1536.0, AD)
         at(t0 + TURN["k"])
-        cp(X("vz", 2, 2163, 144), X("af"))
-        ts(X("bi"), X("rn"), 1.0 / 4096, MU)
-        ts(X("ki"), X("bi"), 15, ALU.bitwise_and)
-        cp(X("vz", 3, 2164, 144), X("ki"))
+        gcp(X("vz", 2, 2163, 144), X("af"))
+        act(X("k1"), X("rn"), bias=-7.5, scale=1.0 / 4096)
+        if KV:
+            ts(X("k2"), X("k1"), MAGIC / 256, AD, MAGIC / 256, SU)
+        else:
+            act(X("k2"), X("k1"), bias=MAGIC / 256)
+            act(X("k2"), X("k2"), bias=-MAGIC / 256)
+        tt(X("vz", 3, 2164, 144), X("k1"), X("k2"), SU)
         for hf in range(2):
-            best = stage(t0 + TURN["s2"][hf], 1, hf, Vt, "co", "coh", ("vcx", 0), ALU.is_gt, AF.Sigmoid, -100.0, 200.0, "blk")
+            best = stage(t0 + TURN["s2"][hf], 1, hf, Vt, "co", "coh", ("vcx", 0, "vc", 0), ALU.is_gt, AF.Sigmoid, -100.0, 200.0, "blk")
             at(t0 + TURN["d2"][hf])
             h = lambda nm: half(nm, hf)
             tt(h("nz"), best, h("hK"), ALU.not_equal)
-            ts(h("nver"), best, 12.0 * 65536 - 1536, ALU.is_ge, -1.0, MU)
-            ts(h("r2"), best, MAGIC, AD, MAGIC, SU)
-            tt(X("vz", 1 + 1152 * hf, 1011 + 1152 * hf, 144), best, h("r2"), SU)
-            na = AOH if hf else 0
-            terms = [(on, half("nz", 0)), (on, half("nver", 0))][:2 * hf] + [(X("U"), h("nz")), (X("U"), h("nver"))]
+            if VERA:
+                act(h("nver"), best, AF.Sigmoid, -11.5 * 8192, 1.0 / 16)
+            else:
+                ts(h("nver"), best, 11.5 * 131072, ALU.is_ge)
+            if not R2MERGE:
+                ts(h("r2"), best, MAGIC, AD, MAGIC, SU)
+                tt(X("vz", 1 + 1152 * hf, 1011 + 1152 * hf, 144), best, h("r2"), SU)
+            elif hf:
+                ts(X("r2"), X("sc1", 15, 272, 17), MAGIC, AD, MAGIC, SU)
+                tt(X("vz", 1, 2162, 144), X("sc1", 15, 272, 17), X("r2"), SU)
+            na = AOH if hf else AOH0
+            terms = [(on, half("nz", 0)), (X("non"), half("nver", 0))][:2 * hf] + [(X("U"), h("nz")), (X("Un"), h("nver"))]
             for bank in ("P2", "P0")[:2 if na else 1]:
                 for i, (l, r) in enumerate(terms):
                     mm(X(bank, 16, 24), l, r, i == 0, i == len(terms) - 1)
             if na:
-                act(X("rp"), X("P0", 16, 24))
+                act(h("rp"), X("P0", 16, 24))
             for gg in range(8 - na, 8):
-                act(X("sq", 64 * gg, 64 * gg + 64), X("io64"), AF.Square, X("rp", gg, gg + 1), -1.0)
+                act(X("sq", 64 * gg, 64 * gg + 64), X("io64"), AF.Square, X("rp", 8 * hf + gg, 8 * hf + gg + 1), -1.0)
             for gg in range(8):
                 i = 8 * hf + gg
                 if gg < 8 - na:
                     ts(X("oh", 64 * i, 64 * i + 64), X("io64"), X("P2", 16 + gg, 17 + gg), EQ)
                 else:
                     act(X("oh", 64 * i, 64 * i + 64), X("sq", 64 * gg, 64 * gg + 64), AF.Relu, 1.0, -1.0)
-                mm(X("P3", 0, 64), X("vz", 128 * gg + 1152 * hf, 128 * gg + 1152 * hf + 128), X("oh", 64 * i, 64 * i + 64), i == 0, i == 15)
+            if hf == 0 and (last or not HSPLIT):
+                continue
+            a, b = (8 * hf, 8 * hf + 8) if HSPLIT and not last else (0, 16)
+            at(t0 + TURN["hn"][hf])
+            held17, hn = X("sc1", 17 * a + 16, 17 * b, 17), X("hn", 16 * t + a, 16 * t + b)
+            ts(X("r3", a, b), held17, MAGIC, AD, MAGIC, SU)
+            tt(hn, held17, X("r3", a, b), SU)
+            if not last:
+                m = b - 8 * TNA
+                if a < m:
+                    tt(X("TN", 16 * a, 16 * m), IND(hn, X("exl", 0, m - a)), X("m256", 0, 16 * (m - a)), MU)
+                for i in range(m, b):
+                    act(X("TF", 16 * i, 16 * i + 16), X("m256", 0, 16), scale=X("hn", 16 * t + i, 16 * t + i + 1))
+                for c in range(a, b, 8):
+                    mm(X("P2", 32 + c, 40 + c), X("TN" if c < m else "TF", 16 * c, 16 * c + 128), X("jj" if c < m else "jf"), True)
+                ts(X("hs", 16 * t + a, 16 * t + b), X("P2", 32 + a, 32 + b), 1536.0, AD)
+                sent = send(1, X("hs", 16 * t + a, 16 * t + b), "hl", 16 * t + 16 + a, "al%d" % (2 * t + hf), "ll")
+        at(t0 + TURN["d2"][1])
+        for i in range(16):
+            o = 128 * (i % 8) + 1152 * (i // 8)
+            mm(X("P3", 0, 64), X("vz", o, o + 128), X("oh", 64 * i, 64 * i + 64), i == 0, i == 15)
         hn = X("hn", 16 * t, 16 * t + 16)
-        at(t0 + TURN["hn"])
-        tt(X("df"), X("vz", 1, 2162, 144), hT, SU)
-        tt(X("dv"), X("df"), X("nver"), MU)
-        tt(hn, hT, X("dv"), SU)
         if not last:
-            tt(X("TN"), IND(hn, X("exl")), X("m256"), MU)
-            for hf in range(2):
-                mm(X("P2", 32 + 8 * hf, 40 + 8 * hf), X("TN", 128 * hf, 128 * hf + 128), X("jj"), True, True)
-            ts(X("hs", 16 * t, 16 * t + 16), X("P2", 32, 48), 1536.0, AD)
-            send(1, X("hs", 16 * t, 16 * t + 16), "hl", 16 * t + 16, "al%d" % (t + 1), "ll")
-            send(1, hn, "hT", 16 * t + 16, "at%d" % (t + 1), "lt")
+            sent = send(1, hn, "hT", 16 * t + 16, "at%d" % (t + 1), "lt", [sent])
+        if t + 2 < S:
+            costs(t + 2, [sent])
         at(t0 + TURN["ho"])
         mm(X("P2", 160, 288, 1, (0, 16)), hn, X("If"), True, True)
         act(X("hob", 128 * t, 128 * t + 128, 1, (0, 16)), X("P2", 160, 288, 1, (0, 16)), AF.Copy, 1536.0)
@@ -376,35 +472,44 @@ def rank_program(g, core, T, topo):
         at(t0 + TURN["x"])
         cp(X("rs16"), X("P3", 0, 64))
         mm(X("P6", 0, 192), X("Ib"), X("mkL", 0, 192), True, False)
-        for v in (1, 0, 2):
-            mm(X("P6", 64 * v, 64 * v + 64), X("se%d" % v), X("rs16"), False, v == 2)
+        for v, nm in enumerate(("se1", "se0", "se2")):
+            mm(X("P6", 64 * v, 64 * v + 64), X(nm), X("rs16"), False, v == 2)
         mm(X("P1", 128, 192), X("se3"), X("rs16"), True, True)
-        scan(X("LS", 64, 128), X("rst", 0, 64), X("P6", 64, 128))
-        cp(X("gl", 4, 8), X("LS", 79, 128, 16))
-        ts(X("K64"), X("P1", 128, 192), X("kcode"), EQ)
-        tt(X("prod"), IND(At, X("gl", 4, 8)), X("K64"), MU)
-        for v in (0, 2):
-            scan(X("LS", 64 * v, 64 * v + 64), X("rst", 0, 64), X("P6", 64 * v, 64 * v + 64))
+        scan(X("LS", 0, 64), X("rst", 0, 64), X("P6", 0, 64))
         cp(X("gl", 0, 4), X("LS", 15, 64, 16))
+        if KA:
+            act(X("kq"), X("P1", 128, 192), AF.Square, X("kcode"), -1.0)
+            act(X("K64"), X("kq"), AF.Relu, 1.0, -1.0)
+        else:
+            ts(X("K64"), X("P1", 128, 192), X("kcode"), EQ)
+        tt(X("prod"), IND(At, X("gl", 0, 4)), X("K64"), MU)
+        scan(X("LS", 64, 192), X("rst"), X("P6", 64, 192))
         mm(X("P0", 64, 128), X("Ib"), X("mkL", 0, 64), True, False)
         mm(X("P0", 64, 128), X("bob"), X("prod"), False, True)
         scan(X("LS", 192, 256), X("rst", 0, 64), X("P0", 64, 128))
-        cp(X("gl", 8, 16), X("LS", 143, 256, 16))
-        for bank, srcs in (("P4", (("se0", "rs16"), ("se1", "rs16"))), ("P5", (("se2", "rs16"), ("bob", "prod")))):
-            mm(X(bank, 0, 320), X("Ib"), X("mkR"), True, False)
+        cp(X("gl", 4, 16), X("LS", 79, 256, 16))
+        nb_ = BPAIR // 2
+        assets = (("se2", "rs16"), ("bob", "prod"))
+        for bank, srcs, q0, q1 in (("P4", (("se0", "rs16"), ("se1", "rs16")), 0, 4), ("P5", assets, 0, 4 - nb_), ("P6", assets, 4 - nb_, 4)):
+            if q0 == q1:
+                continue
+            c0, c1 = blocks[q0][0], blocks[q1 - 1][0] + 2 * blocks[q1 - 1][1]
+            mm(X(bank, c0, c1), X("Ib"), X("mkR", c0, c1), True, False)
             for hh in range(2):
-                for q, (o, wd) in enumerate(blocks):
-                    mm(X(bank, o + hh, o + 2 * wd, 2), X(srcs[hh][0]), X(srcs[hh][1], 16 * q, 64), False, hh == 1 and q == 3)
+                for q in range(q0, q1):
+                    o, wd = blocks[q]
+                    mm(X(bank, o + hh, o + 2 * wd, 2), X(srcs[hh][0]), X(srcs[hh][1], 16 * q, 64), False, hh == 1 and q == q1 - 1)
         mm(X("P7", 0, 128), X("Ib"), X("mkC"), True, False)
         e, pairs = 0, []
         for bank, base in (("P4", 0), ("P5", 128)):
             for q, (o, wd) in enumerate(blocks):
                 for v in range(2):
-                    pairs.append((X(bank, o, o + 2 * wd), X("LS", base + 64 * v + 16 * q + 15, base + 64 * v + 16 * q + 16), e, wd))
+                    src = X("P6" if base and q >= 4 - nb_ else bank, o, o + 2 * wd)
+                    pairs.append((src, X("LS", base + 64 * v + 16 * q + 15, base + 64 * v + 16 * q + 16), e, wd))
                     e += 2 * wd
-        for src, col, e, wd in pairs[APAIR:8] + pairs[8 + BPAIR:]:
+        for src, col, e, wd in pairs[APAIR:16 - BPAIR]:
             ts(X("E", e, e + 2 * wd), src, col, EQ)
-        for part in (pairs[:APAIR], pairs[8:8 + BPAIR]):
+        for part in (pairs[:APAIR], pairs[16 - BPAIR:]):
             for src, col, e, wd in part:
                 act(X("sq", e, e + 2 * wd), src, AF.Square, col, -1.0)
             e0, e1 = (part[0][2], part[-1][2] + 2 * part[-1][3]) if part else (0, 0)
@@ -416,36 +521,38 @@ def rank_program(g, core, T, topo):
         at(t0 + TURN["nw"])
         act(X("vg", 0, 128), IND(Vt, X("gl", 0, 8)))
         act(X("vg", 128, 256), IND(Yt, X("gl", 8, 16)))
-        for o, ya, yb in ((0, "Ib", "Inb"), (64, "Inb", "Ib")):
+        for o, ya, yb in ((0, "Inb", "Ib"), (64, "Ib", "Inb")):
             mm(X("P3", 256 + o, 320 + o), X("Ib"), X("vg", o, o + 64), True, False)
             mm(X("P3", 256 + o, 320 + o), X(ya), X("vg", 128, 192), False, False)
             mm(X("P3", 256 + o, 320 + o), X(yb), X("vg", 192, 256), False, True)
         act(X("nv"), X("P3", 256, 384))
         if not last:
-            mm(X("P1", 256, 320), X("bob"), X("prod"), True, False)
-            mm(X("P1", 256, 320), X("se2n"), X("rs16"), False, True)
-            mm(X("P1", 320, 384), X("sd"), X("rs16"), True, True)
-            for v in range(2):
-                tt(X("KD", 64 * v, 64 * v + 64), X("P1", 256 + 64 * v, 320 + 64 * v), X("K64"), MU)
-            for v in range(4):
+            act(X("ag"), IND(At, X("gl", 0, 8)))
+            for v, (nb1, na1) in enumerate((("bon", "se2"), ("bob", "se2n"))):
+                mm(X("P1", 256 + 64 * v, 320 + 64 * v), X(nb1), X("prod"), True)
+                mm(X("P1", 256 + 64 * v, 320 + 64 * v), X(na1), X("rs16"), False)
+            mm(X("P1", 384, 448), X("sd"), X("rs16"), True)
+            for v in range(3):
                 at(t0 + TURN["upd" if v // 2 else "nw"])
-                tt(X("NW", 64 * v, 64 * v + 64), IND((At, Ot)[v // 2], X("gl", 4 * v, 4 * v + 4)), X("KD", 64 * (v // 2), 64 * (v // 2) + 64), (AD, SU)[v % 2])
+                tt(X("KD", 64 * v, 64 * v + 64), X("P1", 256 + 64 * v, 320 + 64 * v), X("K64"), MU)
+            for v in range(2):
+                tt(X("NW", 64 * v, 64 * v + 64), IND(Ot, X("gl", 8 + 4 * v, 12 + 4 * v)), X("KD", 128, 192), (AD, SU)[v])
         at(t0 + TURN["x"])
         scan(X("PS"), X("r32"), X("P7", 0, 128))
         tt(X("XD"), IND(X("PS"), X("sx", 0, 1)), X("DUM"), ALU.min)
         tt(X("of"), X("XD"), X("LS", 15, 256, 16), ALU.max)
         cp(X("so"), X("of"))
         if not last:
-            cp(IND(X("At"), X("so", 0, 8)), X("NW", 0, 128))
+            tt(IND(X("At"), X("so", 0, 8)), X("ag"), X("KD", 0, 128), AD)
         at(t0 + TURN["vt"])
         cp(IND(X("Vt"), X("so", 0, 8)), X("nv"))
         at(t0 + TURN["upd"])
         if not last:
-            cp(IND(X("Ot"), X("so", 8, 16)), X("NW", 128, 256))
+            cp(IND(X("Ot"), X("so", 8, 16)), X("NW", 0, 128))
     dma("S", (T.vo[:, :], []), Vt)
 
     n = len(calls)
-    delay = lambda a, b: 0.0 if calls[a][0] == calls[b][0] == "P" or calls[b][0] == "R" else WAKE
+    delay = lambda a, b: RCALL - HOPTIME if (a, b) in loose else 0.0 if calls[a][0] == calls[b][0] == "P" or calls[b][0] == "R" else WAKE + XWAKE * (calls[a][0] != calls[b][0])
     after, left = [[] for _ in range(n)], [0] * n
     for i in range(n - 1, 0, -1):
         left[i] = len(calls[i][6])
@@ -485,14 +592,21 @@ def rank_program(g, core, T, topo):
     pre = [[]] + [c[6] for c in calls[1:]]
     span = lambda s: max(s[i] + calls[i][5] for i in range(1, n))
     cur = start
-    for _ in range(ROUNDS):
+    rng = np.random.default_rng(SEED)
+    for r in range(ROUNDS):
+        if JITTER and r >= 2:
+            cur = list(start)
+            jit = (rng.random(n) * JITTER * (rng.random(n) < JFRAC))[kind]
+            for i in range(1, n):
+                cur[i] = max([cur[i] + jit[i]] + [cur[p] + calls[p][4] for p in pre[i]])
         back = justify(sorted(range(1, n), key=lambda i: (-cur[i] - calls[i][4], -i)), after,
-                       lambda p, i: calls[p][4] + calls[i][5] - calls[i][4] + delay(i, p))
+                       lambda p, i: calls[p][4] + calls[i][5] - calls[i][4] + delay(i, p) + MARGIN * (calls[p][0] == "R"))
         cur = justify(sorted(range(1, n), key=lambda i: (-back[i] - calls[i][4], i)), pre, lambda p, i: calls[p][5] + delay(p, i))
         if span(cur) < span(start):
             start = cur
     order = sorted(range(1, n), key=lambda i: (start[i] if calls[i][6] or calls[i][3] != 16 else -1.0, i))
-    cnt, tok, seen, snap = {}, {}, {q: {} for q in Q}, {}
+    closes.update(max(grp, key=lambda i: (start[i], i)) for grp in groups)
+    cnt, tok, seen, snap, issued = {}, {}, {q: {} for q in Q}, {}, {}
     for i in order:
         if calls[i][0] == "R":
             tok[i], snap[i] = (calls[i][2], calls[i][3]), {}
@@ -502,10 +616,14 @@ def rank_program(g, core, T, topo):
         if q == "R":
             continue
         for p in sorted(calls[i][6], key=lambda p: -start[p]):
-            if q == "P" and calls[p][0] == "P":
+            if q == calls[p][0] == "P" or (p, i) in loose:
                 continue
             s, v = tok[p]
             if seen[q].get(s, 0) < v:
+                for j in reversed(issued.get(s, [])):
+                    if tok[j][1] <= v or start[j] + calls[j][5] + DONE <= start[i]:
+                        p, v = (j, tok[j][1]) if tok[j][1] > v else (p, v)
+                        break
                 Q[q].wait_ge(T.sem[s], v)
                 seen[q][s] = v
                 for s2, v2 in snap[p].items():
@@ -513,6 +631,8 @@ def rank_program(g, core, T, topo):
         issue()
         cnt[sem] = cnt.get(sem, 0) + inc
         tok[i], snap[i] = (sem, cnt[sem]), dict(seen[q])
+        if sem == "c" + q:
+            issued.setdefault(sem, []).append(i)
     for sem, v in sorted(cnt.items()):
         if seen["G"].get(sem, 0) < v:
             g.wait_ge(T.sem[sem], v)

import numpy as np
from concourse.mybir import AluOpType as ALU, ActivationFunctionType as AF

N, C, D, S, HOP = 4, 3072, 256, 4, 1
NA = ((48, 72), (80, 40))
CUTS = (((0, 128), (0, 128)), ((0, 128), (0, 128)))
ACHUNK = 32
VCHUNK = 16
CASPLIT, R2MERGE, KA = 0, 0, 0
AOCUT, YCUT = (0, 1024, 2048, C), (0, C)
FIX, XWAKE = 0.01, -0.03
HSPLIT, GCP, MARGIN, LATE = 0, 0, 0.0, 3.0
JITTER, JFRAC, SEED = 0.0, 0.1, 0
DONE, TNA = 0.3, 0
COVER, VERA, NPASS, PEFIX = 0, 1, 6, 0.0
AMUL, AVC, AOH0 = 0.95, 0, 2
AFIX, KV, GMUL, RCALL = 0.025, 1, 1.05, 0.9
STR, VSPLIT, Z0 = (0, 0), 1, "A"
AOH = 0
APAIR, BPAIR, RELU = 8, 0, 256
GZ, GVC = (8, 10), (10, 8)
TURN = dict(ca=(0, 1), s1=(5, 5), d1=(5, 9), s2=(16, 9), d2=(12, 17), vg=3, vc=(3, 11), vt=108, upd=106, k=18, hn=(11, 16), ho=93, x=25, nw=24, zx=40, z1=30, at=24)
AHEAD, PAHEAD, SLACK, ROUNDS = 0.1, 0.2, 0.05, 3
MAGIC = 1.5 * 2.0 ** 35
CYC, PECYC, WAKE, GATHER, SCATTER, HOPTIME, LOADRATE = 0.86e-3, 0.65e-3, 0.21, 1.35, 3.6, 4.0, 500e3
F, B, H, I32, U16 = "float32", "bfloat16", "float16", "int32", "uint16"
SCRATCH = {}
for _n, _w, _d in (
        ("At", C + 128, F), ("Ai", C, I32), ("ag", 128, F), ("bon", 128, B), ("Ot", C + 128, I32), ("Vt", C + 128, B), ("Yt", C, B), ("z0", D, B), ("z", S * D, B), ("zx", S * 16 * D, B),
        ("mn0", 16 * D, B), ("mn1", 16 * D, B), ("gy0", 16 * D, B), ("gy1", 16 * D, B), ("vc", D, B), ("vcx", 16 * D, B),
        ("hdi", 16, I32), ("hdo", 16, F), ("hl", 16 * S, U16), ("hT", 16 * S, F), ("hs", 16 * S, U16), ("hn", 16 * S, F), ("hK", 16, F),
        ("ca", D, U16), ("co", D, U16), ("cah", D, H), ("coh", D, H), ("sc0", D, F), ("sc1", 272, F), ("rn", 16, F), ("af", 16, F), ("k1", 16, F), ("k2", 16, F),
        ("TM", D, H), ("TN", D, H), ("TF", D, F), ("jf", 8, F), ("kq", 64, F), ("la", 16, U16), ("r2", 16, F), ("nver", 16, B), ("nz", 16, B), ("r3", 16, F), ("I17", 136, B), ("b17", 136, B), ("r17", 136, F), ("i17", 136, F), ("rp", 16, F),
        ("vz", 2304, H), ("oh", 1024, B), ("sq", 1280, F), ("rs16", 64, H), ("LS", D, F), ("gl", 16, U16),
        ("K64", 64, F), ("prod", 64, H), ("E", 1280, B), ("KD", 192, F), ("NW", D, I32), ("vg", D, B), ("nv", 128, B),
        ("PS", 128, F), ("XD", 16, F), ("of", 16, F), ("so", 16, U16), ("hob", 512, F),
        ("ipi", 1, I32), ("p16i", 1, I32), ("pgi", 1, I32), ("p16", 1, F), ("pg", 1, F), ("kcode", 1, F), ("sv", 8, F), ("sxi", 2, I32), ("sx", 2, U16),
        ("i128", 128, F), ("ub", 1, F), ("imod", 256, F), ("idiv", 128, B), ("itwo", 128, F), ("r32", 128, F), ("DUM", 16, F),
        ("If", 128, F), ("Ib", 128, B), ("Inb", 128, B), ("U", 128, B), ("Un", 128, B), ("non", 128, B), ("on", 128, B), ("m256", 256, F), ("bo", 128, F),
        ("boh", 128, B), ("jj", 8, B), ("blk", 8, B), ("nblk", 8, B), ("rst", 128, F), ("brow", 128, B), ("cl", 256, B), ("cr", 128, B),
        ("io64", 64, B), ("exl", 16, U16), ("bob", 128, B), ("mkL", 192, B), ("mkC", 128, B), ("mkR", 320, B),
        ("se0", 128, B), ("se1", 128, B), ("se2", 128, B), ("se3", 128, B), ("se4n", 128, B), ("se2n", 128, B), ("sd", 128, B)):
    SCRATCH[_n] = ("sbuf", [128, _w], _d)
for _i in range(8):
    SCRATCH["P%d" % _i] = ("psum", [128, 512], F)
SEMAPHORES = (["cV", "cA", "cP", "cG"] + ["d%d" % i for i in range(32)] + ["a%s%d" % (k, i) for k in "zt" for i in (1, 2, 3)] + ["al%d" % i for i in range(6)] + ["lz", "ll", "lt"])


def rank_program(g, core, T, topo):
    rank = T.rank_of(core)
    if rank is None:
        return
    Q = {"V": g.vector, "A": g.scalar, "P": g.tensor, "G": g, "S": g.sync}
    calls = [None]
    Wr, Rd = {}, {}
    held, turn, raw = {}, [0.0], {}
    nth, kinds, kind = {}, {}, [0]

    def record(q, issue, sem, n, hold, lat, reads, writes, after=(), free=False):
        pre = set(after)
        me = len(calls)
        names = [x[0] for x in writes + reads] or [""]
        for name, cols in reads + writes:
            if name not in Wr:
                Wr[name] = np.zeros(SCRATCH[name][1][1], np.int64)
                Rd[name] = []
        banks = {nm for nm, _ in reads + writes if SCRATCH[nm][0] == "psum"}
        for name in banks:
            users = Rd[name]
            if free:
                pre.add(users[0])
            elif q == "P" or any(calls[u][0] != q for u in users):
                held[name], Rd[name] = users, []
            pre.update(held.get(name, []))
            Rd[name].append(me)
        reads, writes = [x for x in reads if x[0] not in banks], [x for x in writes if x[0] not in banks]
        raw[me] = set()
        for name, cols in reads:
            raw[me].update(Wr[name][cols].tolist())
        pre.update(raw[me])
        for name, cols in writes:
            pre.update(set(Wr[name][cols].tolist()))
            pre.update(r for r, m in Rd[name] if m[cols].any())
            Wr[name][cols] = me
            for r, m in Rd[name]:
                m[cols] = False
            Rd[name] = [x for x in Rd[name] if x[1].any()]
        for name, cols in reads:
            m = np.zeros(len(Wr[name]), bool)
            m[cols] = True
            Rd[name].append((me, m))
        pre.discard(0)
        pre.discard(me)
        key = (q, names[0], names[-1])
        nth[key] = nth.get(key, 0) + 1
        kind.append(kinds.setdefault(key + (nth[key],), len(kinds)))
        calls.append([q, issue, sem, n, hold, lat, pre, turn[0]])
        return me

    def at(x):
        turn[0] = x

    def op(q, call, writes, reads, cost, free=False):
        record(q, lambda: call().then_inc(T.sem["c" + q], 1), "c" + q, 1, cost, cost,
               [a for x in reads for a in x[1]], [a for x in writes for a in x[1]], free=free)

    def X(name, a=None, b=None, s=1, p=None):
        a = 0 if a is None else a
        b = SCRATCH[name][1][1] if b is None else b
        ps = slice(None) if p is None else slice(p[0], p[1])
        ap = T[name][ps, a:b] if s == 1 else T[name][ps, a:b:s]
        return (ap, [(name, slice(a, b, s))], len(range(a, b, s)), SCRATCH[name][2] in (B, H, U16), SCRATCH[name][0] == "psum", False)

    def IND(win, off):
        return (win[0].indirect(off[0]), win[1] + off[1], 16 * off[2], False, False, True)

    def vcost(o, i, rate):
        if o[5] or i[5]:
            return FIX + 0.06 + i[2] * (SCATTER if o[5] else GATHER) * CYC
        return FIX + max(64, i[2] * rate) * CYC

    def cp(o, i):
        if o[5]:
            op("V", lambda: g.vector.tensor_copy(o[0], i[0]), [(0, o[1][:1])], [i, (0, o[1][1:])], vcost(o, i, 1))
        else:
            op("V", lambda: g.vector.tensor_copy(o[0], i[0]), [o], [i], vcost(o, i, 0.5 if o[3] and i[3] else 1))

    def tt(o, a, b, f):
        op("V", lambda: g.vector.tensor_tensor(o[0], a[0], b[0], f), [(0, o[1][:1])], [a, b, (0, o[1][1:])], vcost(o, a, 1 if a[4] or b[4] else 2))

    def val(x, rs):
        if isinstance(x, tuple):
            rs.append(x)
            return x[0]
        return x

    def ts(o, a, s1, f1, s2=None, f2=None):
        rs = [a]
        v1, v2 = val(s1, rs), val(s2, rs)
        cost = vcost(o, a, 0.5 if o[3] and a[3] else 1)
        if f2 is None:
            op("V", lambda: g.vector.tensor_scalar(o[0], a[0], v1, None, f1), [o], rs, cost)
        else:
            op("V", lambda: g.vector.tensor_scalar(o[0], a[0], v1, v2, f1, f2), [o], rs, cost)

    def fill(o, c):
        op("V", lambda: g.vector.memset(o[0], c), [o], [], vcost(o, o, 0.5 if o[3] else 1))

    def scan(o, d0, d1):
        op("V", lambda: g.vector.tensor_tensor_scan(o[0], d0[0], d1[0], 0.0, ALU.mult, ALU.max), [o], [d0, d1], vcost(o, d1, 1))

    def act(o, i, f=AF.Copy, bias=0.0, scale=1.0):
        rs = [i]
        b, c = val(bias, rs), val(scale, rs)
        op("A", lambda: g.scalar.activation(o[0], i[0], f, bias=b, scale=c), [o], rs, vcost(o, i, 1) * AMUL + AFIX)

    groups, closes = [], set()

    def mm(o, l, r, start, stop=None, chain=False):
        me = len(calls)
        if start:
            groups.append([])
            opened[o[1][0][0]] = groups[-1]
        opened[o[1][0][0]].append(me)
        op("P", lambda: g.tensor.matmul(o[0], l[0], r[0], start, me in closes), [o], [l, r],
           max(min(64, l[2]), r[2]) * (1 if l[3] else 4) * PECYC + PEFIX, not start and not chain)
    opened = {}

    def iota(o, pat, base, cm):
        cost = 0.14 + 2 * o[2] * CYC
        if SCRATCH[o[1][0][0]][2] == I32:
            op("G", lambda: g.iota(o[0], pat, base, cm), [o], [], cost)
        else:
            op("G", lambda: g.iota(o[0], pat, base, cm, allow_small_or_imprecise_dtypes=True), [o], [], cost)

    def sel(o, i, pat, f, c, base, cm):
        op("G", lambda: g.affine_select(o[0], i[0], pat, f, c, base, cm), [o], [i], (0.18 + 2 * o[2] * CYC) * GMUL)

    def gcp(o, i):
        if GCP:
            sel(o, i, [[0, o[2]]], ALU.is_ge, 0.0, 0, 0)
        else:
            cp(o, i)

    nd, loaded = [0], [2.0]

    def dma(q, o, i, nbytes=0):
        sem = "d%d" % nd[0]
        nd[0] += 1
        loaded[0] += nbytes / LOADRATE
        record(q, lambda: Q[q].dma_start(o[0], i[0]).then_inc(T.sem[sem], 16), sem, 16, 0.05, loaded[0] if nbytes else 2.0, i[1], o[1])

    def send(hops, src, name, a, rsem, lsem, behind=()):
        dst, frm = T.cores[(rank + hops * HOP) % N], T.cores[(rank - hops * HOP) % N]
        rid, pid, _ = topo.addr(dst)
        eng = topo.engines(core, dst)[:8]
        s = record("G", lambda: g.remote_dma(T[name][:, a:a + src[2]], src[0], T.sem[rsem], T.sem[lsem], pid, rid, sum(1 << e for e in eng)),
                   lsem, len(eng), RCALL, HOPTIME, src[1], [], behind)
        loose.update((p, s) for p in behind)
        record("R", None, rsem, len(topo.engines(frm, core)[:8]), 0.0, LATE if name != "hl" else 0.0, [], X(name, a, a + src[2])[1], [s])
        return s
    loose = set()

    EQ, MU, AD, SU = ALU.is_equal, ALU.mult, ALU.add, ALU.subtract
    dma("S", X("hdi"), (T.hd[:, :], []))
    dma("A", X("z0"), (T.zc[:, :], []))
    i = 0
    for nm, src, size, cuts in (("Ot", T.ao, 512, AOCUT), ("Yt", T.yd, 256, YCUT), ("Vt", T.ve, 256, (0, C))):
        for a, b in zip(cuts, cuts[1:]):
            dma("S", X(nm, a, b), (src[:, a:b], []), size * (b - a))
            i += 1
    act(X("z", 0, D), X("z0"), scale=-1.0)
    for r in range(1, N):
        send(r, X("z", 0, D), "z", r * D, "az%d" % r, "lz")
    on = X("on")
    iota(X("ipi"), [[0, 1]], 0, 1)
    iota(X("i128"), [[1, 128]], 0, 0)
    iota(X("imod"), [[0, 16], [1, 16]], 0, 0)
    iota(X("idiv"), [[1, 8], [0, 16]], 0, 0)
    iota(X("itwo"), [[0, 4], [1, 16], [0, 2]], 0, 0)
    iota(X("r32"), [[0, 4], [1, 32]], 0, 0)
    iota(X("DUM"), [[0, 2], [16, 8]], C, 0)
    iota(X("io64"), [[1, 64]], 1 - 256, 0)
    fill(on, 1.0)
    fill(X("vz"), 0.0)
    fill(X("vz", 4, 2165, 144), 1.0)
    sel(X("Ib"), on, [[-1, 128]], EQ, 0.0, 0, 1)
    p16, pg = X("p16"), X("pg")
    ts(X("p16i"), X("ipi"), 15, ALU.bitwise_and)
    ts(X("pgi"), X("ipi"), 4, ALU.logical_shift_right)
    ts(X("sxi", 0, 1), X("ipi"), 3, ALU.bitwise_and)
    ts(X("ub"), X("ipi"), -200.0, MU, 100.0, AD)
    cp(p16, X("p16i"))
    cp(pg, X("pgi"))
    ts(X("sx", 0, 1), X("sxi", 0, 1), 32.0, MU, 31.0, AD)
    cp(X("hl", 0, 16), X("hdi"))
    ts(X("hdo"), X("hdi"), -1536.0, AD)
    ts(X("jj"), X("i128", 0, 8), pg, EQ)
    cp(X("exl"), X("i128", 0, 16))
    ts(X("m256"), X("imod"), p16, EQ)
    ts(X("DUM"), X("DUM"), p16, AD)
    act(X("U"), X("i128"), AF.Sigmoid, X("ub"), 200.0)
    sel(X("U"), X("U"), [[1, 128]], ALU.not_equal, -255.0, 0, -1)
    act(X("Un"), X("U"), scale=-1.0)
    act(X("non"), on, scale=-1.0)
    act(X("If"), X("Ib"))
    act(X("Inb"), X("Ib"), scale=-1.0)
    act(X("brow"), X("imod", 0, 128), bias=61440.0, scale=-4096.0)
    act(X("rst"), X("imod", 0, 128), AF.Sign)
    act(X("r32"), X("r32"), AF.Sign)
    iota(X("i17"), [[0, 8], [1, 17]], 0, 0)
    act(X("r17"), X("i17"), AF.Sign)
    act(X("b17"), X("i17"), bias=61440.0, scale=-4096.0)
    fill(X("b17", 16, 136, 17), 11.75 * 131072)
    fill(X("I17"), 1.0)
    sel(X("I17"), X("I17"), [[-16, 8], [-1, 17]], EQ, 0.0, 0, 1)
    fill(X("I17", 16, 136, 17), 0.0)
    for nm, c in (("blk", 131072.0), ("nblk", -65536.0), ("jf", 1.0)):
        act(X(nm), X("jj"), scale=c)
    act(X("kcode"), p16, bias=7.5, scale=-1.0)
    row = [[-16, 8], [0, 16]]
    for nm, v, c in (("se0", 0, 1.0), ("se1", 1, 1.0), ("se2", 2, 1.0), ("se3", 3, 1.0), ("se4n", 4, -8192.0), ("se2n", 2, -1.0), ("sd", 1, 4096.0)):
        if c != 1.0:
            fill(X(nm), c)
        sel(X(nm), X(nm) if c != 1.0 else on, row, EQ, 0.0, -v, 1)
    sel(X("sd"), X("sd"), row, ALU.not_equal, -4096.0, 0, 1)
    for nm, c in (("bob", 1.0), ("boh", 8192.0), ("bon", -1.0)):
        ts(X(nm), X("idiv"), pg, EQ, c, MU)
    act(X("mkL"), X("m256", 0, 192), bias=-16384.0, scale=16384.0 + 1536.0)
    for hh in range(2):
        act(X("mkC", hh, 128, 2), X("m256", 0, 64), bias=-2.0 ** 22, scale=2.0 ** 22 + 8192.0 * (1 - hh))
    blocks = [(0, 64), (128, 48), (224, 32), (288, 16)]
    fill(X("mkR"), 1536.0)
    ts(X("mkR", 0, 32), X("itwo", 0, 32), p16, ALU.is_le, 16384.0, MU)
    act(X("mkR", 0, 32), X("mkR", 0, 32), bias=1536.0)
    for o, wd in blocks[1:]:
        act(X("mkR", o, o + 32), X("mkR", 0, 32))
    two = (0, 2)
    sel(X("cr", p=two), X("brow", p=two), [[0, 128]], EQ, 240.0 * 65536, 0, 1)
    sel(X("cl", 0, 128, 1, two), X("on", p=two), [[-1, 128]], ALU.is_ge, 0.0, NA[0][0] + 999, -1000)
    sel(X("cl", 128, 256, 1, two), X("on", p=two), [[1, 128]], ALU.is_ge, 0.0, NA[0][1] + 872, -1000)
    for a, b in zip(YCUT, YCUT[1:]):
        m = a + (b - a) * 2 // 3
        ts(X("Yt", a, m), X("Yt", a, m), -1.0, MU)
        act(X("Yt", m, b), X("Yt", m, b), scale=-1.0)
    at(TURN["at"])
    w = C // NPASS
    for a in range(0, C, w):
        ts(X("Ai", a, a + w), X("Ot", a, a + w), 4095, ALU.bitwise_and)
        ts(X("At", a, a + w), X("Ai", a, a + w), -1536.0, AD)
    at(0)
    At, Ot, Vt, Yt = X("At", 0, C), X("Ot", 0, C), X("Vt", 0, C), X("Yt")

    half = lambda nm, hf, t=0: X(nm, 16 * t + 8 * hf, 16 * t + 8 * hf + 8)

    def conv(src, tm, hf, out):
        tt(X(tm, 128 * hf, 128 * hf + 128), IND(src, X("exl", 0, 8)), X("m256", 0, 128), MU)
        mm(out, X(tm, 128 * hf, 128 * hf + 128), X("jj"), True, True)

    def spread(how, dst, src, a, b, ks):
        for k in ks:
            o, i = X(dst, 16 * a + k, 16 * b, 16), X(src, a, b)
            if how == "G":
                sel(o, i, [[0, b - a]], ALU.is_ge, 0.0, 0, 0)
            else:
                (act if how == "A" else cp)(o, i)

    nb = [0]

    def stage(t0, st, hf, win, lst, lsth, other, f, func, bias, scale, wt):
        bank, mn, gy, mo = "P%d" % hf, "mn%d" % st, "gy%d" % st, 128 * hf
        wide = lambda nm, a, b: X(nm, 16 * a, 16 * b)
        oth = lambda a, b: X(other[0], other[1] + 16 * a, other[1] + 16 * b)
        at(t0)
        W = 16 + st
        mm(X(bank, 0, 8 * W), X(lsth, mo, mo + 128), X(("Ib", "I17")[st]), True, False)
        if st:
            mm(X(bank, 16, 8 * W, W), X("Ib"), X("vz", 1152 * hf, 1010 + 1152 * hf, 144), False, False)
        a0, v0 = (mo, mo + NA[st][0]) if hf == 0 else (D - NA[st][1], D)
        got = 0
        for a in range(a0, v0, 32):
            b = min(v0, a + 32)
            pb = X("P%d" % (4 + nb[0] % 4), 0, 16 * (b - a))
            nb[0] += 1
            if a >= got:
                got = v0 if v0 - a <= ACHUNK else b
                act(wide(gy, a, got), IND(win, X(lst, a, got)))
            s0, s1 = SPREAD[st]
            if s0 <= a and b <= s1:
                mm(pb, X("Inb"), oth(a, b), True)
                mm(pb, X("Ib"), wide(gy, a, b), False)
            else:
                if COVER:
                    mm(pb, X("Ib"), wide(gy, a, b), True)
                for k in range(16):
                    mm(X(pb[1][0][0], k, 16 * (b - a), 16), X("Inb"), X(other[2], other[3] + a, other[3] + b), k == 0 and not COVER, chain=True)
                if not COVER:
                    mm(pb, X("Ib"), wide(gy, a, b), False, chain=True)
            act(wide(mn, a, b), pb, func, bias, scale)
        v0, v1 = (v0, mo + 128) if hf == 0 else (mo, a0)
        for a in range(v0, v1, VCHUNK):
            b = min(v1, a + VCHUNK)
            tt(wide(mn, a, b), IND(win, X(lst, a, b)), oth(a, b), f)
        for d0, d1 in zip(CUTS[st][hf], CUTS[st][hf][1:]):
            for k in range(16):
                mm(X(bank, k, 8 * W, W, (d0, d1)), X(mn, 16 * (mo + d0) + k, 16 * (mo + d1), 16), X(wt), False, False)
        rows = (0, 2 - st)
        mm(X(bank, 0, 8 * W), X("cl", mo, mo + 128, 1, rows), X(("cr", "b17")[st], p=rows), False, chain=len(CUTS[st][hf]) > 2)
        scan(X("sc%d" % st, 8 * W * hf, 8 * W * (hf + 1)), X(("rst", "r17")[st]), X(bank, 0, 8 * W))
        return X("sc%d" % st, 8 * W * hf + 15, 8 * W * (hf + 1), W)

    SPREAD = [(NA[st][0] * (STR[st] > 0), D - NA[st][1] * (STR[st] > 1)) for st in range(2)]
    spread(Z0, "zx", "z", SPREAD[0][0], SPREAD[0][1], range(16))
    for hf in range(2):
        conv(half("hdo", hf), "TN", hf, X("P2", 8 * hf, 8 * hf + 8))
    cp(X("hT", 0, 16), X("P2", 0, 16))

    def costs(t, behind=()):
        at(100 * (t - 2) + TURN["zx"] if t > 1 else TURN["z1"])
        first = len(calls)
        spread("G", "zx", "z", D * t + SPREAD[0][0], D * t + SPREAD[0][1], range(GZ[t > 1]))
        for i in range(first, len(calls)):
            calls[i][6].update(behind)
            loose.update((p, i) for p in behind)
        spread("A", "zx", "z", D * t + SPREAD[0][0], D * t + SPREAD[0][1], range(GZ[t > 1], 16))
    costs(1)
    for t in range(S):
        last, t0 = t == S - 1, 100 * t
        nth.clear()
        hT = X("hT", 16 * t, 16 * t + 16)
        for hf in range(2):
            at(t0 + TURN["ca"][hf])
            for a, b in ((0, 2), (2, 8)) if hf == 0 and CASPLIT else ((8 * hf, 8 * hf + 8),):
                if t:
                    ts(X("ca", 16 * a, 16 * b), IND(At, X("hl", 16 * t + a, 16 * t + b)), 1536.0, AD)
                else:
                    ts(X("NW", 16 * a, 16 * b), IND(Ot, X("hl", a, b)), 4095, ALU.bitwise_and)
                    cp(X("ca", 16 * a, 16 * b), X("NW", 16 * a, 16 * b))
            at(t0 + TURN["s1"][hf])
            ts(X("cah", 128 * hf, 128 * hf + 128), X("ca", 128 * hf, 128 * hf + 128), -1536.0, AD)
        at(t0 + TURN["vg"])
        act(X("vc"), IND(Vt, X("hl", 16 * t, 16 * t + 16)))
        s0, s1 = SPREAD[1]
        for hf, (a, b) in enumerate(((s0, 128), (128, s1)) if VSPLIT else ((s0, s1),)):
            at(t0 + TURN["vc"][hf])
            spread("G", "vcx", "vc", a, b, range(GVC[hf]))
            spread("A", "vcx", "vc", a, b, range(GVC[hf], GVC[hf] + AVC))
            spread("V", "vcx", "vc", a, b, range(GVC[hf] + AVC, 16))
        at(t0 + TURN["k"])
        gcp(X("vz", 0, 2161, 144), hT)
        act(X("hK"), hT, bias=61440.0)
        for hf in range(2):
            best = stage(t0 + TURN["s1"][hf], 0, hf, Yt, "ca", "cah", ("zx", 16 * D * t, "z", D * t), ALU.max, AF.Relu, 0.0, 1.0, "nblk")
            at(t0 + TURN["d1"][hf])
            ts(half("rn", hf), best, MAGIC, AD, MAGIC, SU)
            tt(half("af", hf), best, half("rn", hf), SU)
            conv(half("af", hf), "TM", hf, X("P2", 8 * hf, 8 * hf + 8))
            ts(half("la", hf), X("P2", 8 * hf, 8 * hf + 8), 1536.0, AD)
            ts(X("co", 128 * hf, 128 * hf + 128), IND(Ot, half("la", hf)), 1.0 / 4096, MU, -0.375, AD)
            ts(X("coh", 128 * hf, 128 * hf + 128), X("co", 128 * hf, 128 * hf + 128), -1536.0, AD)
        at(t0 + TURN["k"])
        gcp(X("vz", 2, 2163, 144), X("af"))
        act(X("k1"), X("rn"), bias=-7.5, scale=1.0 / 4096)
        if KV:
            ts(X("k2"), X("k1"), MAGIC / 256, AD, MAGIC / 256, SU)
        else:
            act(X("k2"), X("k1"), bias=MAGIC / 256)
            act(X("k2"), X("k2"), bias=-MAGIC / 256)
        tt(X("vz", 3, 2164, 144), X("k1"), X("k2"), SU)
        for hf in range(2):
            best = stage(t0 + TURN["s2"][hf], 1, hf, Vt, "co", "coh", ("vcx", 0, "vc", 0), ALU.is_gt, AF.Sigmoid, -100.0, 200.0, "blk")
            at(t0 + TURN["d2"][hf])
            h = lambda nm: half(nm, hf)
            tt(h("nz"), best, h("hK"), ALU.not_equal)
            if VERA:
                act(h("nver"), best, AF.Sigmoid, -11.5 * 8192, 1.0 / 16)
            else:
                ts(h("nver"), best, 11.5 * 131072, ALU.is_ge)
            if not R2MERGE:
                ts(h("r2"), best, MAGIC, AD, MAGIC, SU)
                tt(X("vz", 1 + 1152 * hf, 1011 + 1152 * hf, 144), best, h("r2"), SU)
            elif hf:
                ts(X("r2"), X("sc1", 15, 272, 17), MAGIC, AD, MAGIC, SU)
                tt(X("vz", 1, 2162, 144), X("sc1", 15, 272, 17), X("r2"), SU)
            na = AOH if hf else AOH0
            terms = [(on, half("nz", 0)), (X("non"), half("nver", 0))][:2 * hf] + [(X("U"), h("nz")), (X("Un"), h("nver"))]
            for bank in ("P2", "P0")[:2 if na else 1]:
                for i, (l, r) in enumerate(terms):
                    mm(X(bank, 16, 24), l, r, i == 0, i == len(terms) - 1)
            if na:
                act(h("rp"), X("P0", 16, 24))
            for gg in range(8 - na, 8):
                act(X("sq", 64 * gg, 64 * gg + 64), X("io64"), AF.Square, X("rp", 8 * hf + gg, 8 * hf + gg + 1), -1.0)
            for gg in range(8):
                i = 8 * hf + gg
                if gg < 8 - na:
                    ts(X("oh", 64 * i, 64 * i + 64), X("io64"), X("P2", 16 + gg, 17 + gg), EQ)
                else:
                    act(X("oh", 64 * i, 64 * i + 64), X("sq", 64 * gg, 64 * gg + 64), AF.Relu, 1.0, -1.0)
            if hf == 0 and (last or not HSPLIT):
                continue
            a, b = (8 * hf, 8 * hf + 8) if HSPLIT and not last else (0, 16)
            at(t0 + TURN["hn"][hf])
            held17, hn = X("sc1", 17 * a + 16, 17 * b, 17), X("hn", 16 * t + a, 16 * t + b)
            ts(X("r3", a, b), held17, MAGIC, AD, MAGIC, SU)
            tt(hn, held17, X("r3", a, b), SU)
            if not last:
                m = b - 8 * TNA
                if a < m:
                    tt(X("TN", 16 * a, 16 * m), IND(hn, X("exl", 0, m - a)), X("m256", 0, 16 * (m - a)), MU)
                for i in range(m, b):
                    act(X("TF", 16 * i, 16 * i + 16), X("m256", 0, 16), scale=X("hn", 16 * t + i, 16 * t + i + 1))
                for c in range(a, b, 8):
                    mm(X("P2", 32 + c, 40 + c), X("TN" if c < m else "TF", 16 * c, 16 * c + 128), X("jj" if c < m else "jf"), True)
                ts(X("hs", 16 * t + a, 16 * t + b), X("P2", 32 + a, 32 + b), 1536.0, AD)
                sent = send(1, X("hs", 16 * t + a, 16 * t + b), "hl", 16 * t + 16 + a, "al%d" % (2 * t + hf), "ll")
        at(t0 + TURN["d2"][1])
        for i in range(16):
            o = 128 * (i % 8) + 1152 * (i // 8)
            mm(X("P3", 0, 64), X("vz", o, o + 128), X("oh", 64 * i, 64 * i + 64), i == 0, i == 15)
        hn = X("hn", 16 * t, 16 * t + 16)
        if not last:
            sent = send(1, hn, "hT", 16 * t + 16, "at%d" % (t + 1), "lt", [sent])
        if t + 2 < S:
            costs(t + 2, [sent])
        at(t0 + TURN["ho"])
        mm(X("P2", 160, 288, 1, (0, 16)), hn, X("If"), True, True)
        act(X("hob", 128 * t, 128 * t + 128, 1, (0, 16)), X("P2", 160, 288, 1, (0, 16)), AF.Copy, 1536.0)
        for hf in range(2):
            c0 = t * D + hf * 128
            dma("S", (T.ho[:, c0:c0 + 128], []), X("hob", 128 * t, 128 * t + 128, 1, (8 * hf, 8 * hf + 8)))
        at(t0 + TURN["x"])
        cp(X("rs16"), X("P3", 0, 64))
        mm(X("P6", 0, 192), X("Ib"), X("mkL", 0, 192), True, False)
        for v, nm in enumerate(("se1", "se0", "se2")):
            mm(X("P6", 64 * v, 64 * v + 64), X(nm), X("rs16"), False, v == 2)
        mm(X("P1", 128, 192), X("se3"), X("rs16"), True, True)
        scan(X("LS", 0, 64), X("rst", 0, 64), X("P6", 0, 64))
        cp(X("gl", 0, 4), X("LS", 15, 64, 16))
        if KA:
            act(X("kq"), X("P1", 128, 192), AF.Square, X("kcode"), -1.0)
            act(X("K64"), X("kq"), AF.Relu, 1.0, -1.0)
        else:
            ts(X("K64"), X("P1", 128, 192), X("kcode"), EQ)
        tt(X("prod"), IND(At, X("gl", 0, 4)), X("K64"), MU)
        scan(X("LS", 64, 192), X("rst"), X("P6", 64, 192))
        mm(X("P0", 64, 128), X("Ib"), X("mkL", 0, 64), True, False)
        mm(X("P0", 64, 128), X("bob"), X("prod"), False, True)
        scan(X("LS", 192, 256), X("rst", 0, 64), X("P0", 64, 128))
        cp(X("gl", 4, 16), X("LS", 79, 256, 16))
        nb_ = BPAIR // 2
        assets = (("se2", "rs16"), ("bob", "prod"))
        for bank, srcs, q0, q1 in (("P4", (("se0", "rs16"), ("se1", "rs16")), 0, 4), ("P5", assets, 0, 4 - nb_), ("P6", assets, 4 - nb_, 4)):
            if q0 == q1:
                continue
            c0, c1 = blocks[q0][0], blocks[q1 - 1][0] + 2 * blocks[q1 - 1][1]
            mm(X(bank, c0, c1), X("Ib"), X("mkR", c0, c1), True, False)
            for hh in range(2):
                for q in range(q0, q1):
                    o, wd = blocks[q]
                    mm(X(bank, o + hh, o + 2 * wd, 2), X(srcs[hh][0]), X(srcs[hh][1], 16 * q, 64), False, hh == 1 and q == q1 - 1)
        mm(X("P7", 0, 128), X("Ib"), X("mkC"), True, False)
        e, pairs = 0, []
        for bank, base in (("P4", 0), ("P5", 128)):
            for q, (o, wd) in enumerate(blocks):
                for v in range(2):
                    src = X("P6" if base and q >= 4 - nb_ else bank, o, o + 2 * wd)
                    pairs.append((src, X("LS", base + 64 * v + 16 * q + 15, base + 64 * v + 16 * q + 16), e, wd))
                    e += 2 * wd
        for src, col, e, wd in pairs[APAIR:16 - BPAIR]:
            ts(X("E", e, e + 2 * wd), src, col, EQ)
        for part in (pairs[:APAIR], pairs[16 - BPAIR:]):
            for src, col, e, wd in part:
                act(X("sq", e, e + 2 * wd), src, AF.Square, col, -1.0)
            e0, e1 = (part[0][2], part[-1][2] + 2 * part[-1][3]) if part else (0, 0)
            for e in range(e0, e1, RELU):
                act(X("E", e, min(e1, e + RELU)), X("sq", e, min(e1, e + RELU)), AF.Relu, 1.0, -1.0)
        for src, col, e, wd in pairs:
            mm(X("P7", 128 - 2 * wd, 128), X("boh"), X("E", e, e + 2 * wd), False, False)
        mm(X("P7", 0, 128, 2), X("se4n"), X("rs16"), False, True)
        at(t0 + TURN["nw"])
        act(X("vg", 0, 128), IND(Vt, X("gl", 0, 8)))
        act(X("vg", 128, 256), IND(Yt, X("gl", 8, 16)))
        for o, ya, yb in ((0, "Inb", "Ib"), (64, "Ib", "Inb")):
            mm(X("P3", 256 + o, 320 + o), X("Ib"), X("vg", o, o + 64), True, False)
            mm(X("P3", 256 + o, 320 + o), X(ya), X("vg", 128, 192), False, False)
            mm(X("P3", 256 + o, 320 + o), X(yb), X("vg", 192, 256), False, True)
        act(X("nv"), X("P3", 256, 384))
        if not last:
            act(X("ag"), IND(At, X("gl", 0, 8)))
            for v, (nb1, na1) in enumerate((("bon", "se2"), ("bob", "se2n"))):
                mm(X("P1", 256 + 64 * v, 320 + 64 * v), X(nb1), X("prod"), True)
                mm(X("P1", 256 + 64 * v, 320 + 64 * v), X(na1), X("rs16"), False)
            mm(X("P1", 384, 448), X("sd"), X("rs16"), True)
            for v in range(3):
                at(t0 + TURN["upd" if v // 2 else "nw"])
                tt(X("KD", 64 * v, 64 * v + 64), X("P1", 256 + 64 * v, 320 + 64 * v), X("K64"), MU)
            for v in range(2):
                tt(X("NW", 64 * v, 64 * v + 64), IND(Ot, X("gl", 8 + 4 * v, 12 + 4 * v)), X("KD", 128, 192), (AD, SU)[v])
        at(t0 + TURN["x"])
        scan(X("PS"), X("r32"), X("P7", 0, 128))
        tt(X("XD"), IND(X("PS"), X("sx", 0, 1)), X("DUM"), ALU.min)
        tt(X("of"), X("XD"), X("LS", 15, 256, 16), ALU.max)
        cp(X("so"), X("of"))
        if not last:
            tt(IND(X("At"), X("so", 0, 8)), X("ag"), X("KD", 0, 128), AD)
        at(t0 + TURN["vt"])
        cp(IND(X("Vt"), X("so", 0, 8)), X("nv"))
        at(t0 + TURN["upd"])
        if not last:
            cp(IND(X("Ot"), X("so", 8, 16)), X("NW", 0, 128))
    dma("S", (T.vo[:, :], []), Vt)

    n = len(calls)
    delay = lambda a, b: RCALL - HOPTIME if (a, b) in loose else 0.0 if calls[a][0] == calls[b][0] == "P" or calls[b][0] == "R" else WAKE + XWAKE * (calls[a][0] != calls[b][0])
    after, left = [[] for _ in range(n)], [0] * n
    for i in range(n - 1, 0, -1):
        left[i] = len(calls[i][6])
        for p in calls[i][6]:
            after[p].append(i)
            calls[p][7] = min(calls[p][7], calls[i][7])
    start, ready, idle, order = [0.0] * n, [0.0] * n, {q: 0.0 for q in "VAPGSR"}, []
    cand = {q: [i for i in range(1, n) if calls[i][0] == q and not left[i]] for q in idle}
    while len(order) < n - 1:
        t0, q = min((max(idle[q], min(ready[i] for i in cand[q])), q) for q in cand if cand[q])
        i = min((calls[i][7], i) for i in cand[q] if ready[i] <= t0 + (AHEAD if q in "VA" else PAHEAD))[1]
        if ready[i] > t0:
            i = min([(calls[j][7], j) for j in cand[q] if ready[j] <= t0 and t0 + calls[j][4] <= ready[i] + SLACK] or [(0, i)])[1]
        cand[q].remove(i)
        order.append(i)
        start[i] = max(t0, ready[i])
        idle[q] = start[i] + calls[i][4]
        for j in after[i]:
            ready[j] = max(ready[j], start[i] + calls[i][5] + delay(i, j))
            left[j] -= 1
            if not left[j]:
                cand[calls[j][0]].append(j)

    def justify(order, before, gap):
        at_, busy = [0.0] * n, {q: [] for q in idle}
        for i in order:
            t, slots, hold = max([at_[p] + gap(p, i) for p in before[i]] + [0.0]), busy[calls[i][0]], calls[i][4]
            k = len(slots)
            while k and slots[k - 1][1] > t:
                k -= 1
            while k < len(slots) and t + hold > slots[k][0] + 1e-9:
                t = max(t, slots[k][1])
                k += 1
            slots.insert(k, (t, t + hold))
            at_[i] = t
        return at_
    pre = [[]] + [c[6] for c in calls[1:]]
    span = lambda s: max(s[i] + calls[i][5] for i in range(1, n))
    cur = start
    rng = np.random.default_rng(SEED)
    for r in range(ROUNDS):
        if JITTER and r >= 2:
            cur = list(start)
            jit = (rng.random(n) * JITTER * (rng.random(n) < JFRAC))[kind]
            for i in range(1, n):
                cur[i] = max([cur[i] + jit[i]] + [cur[p] + calls[p][4] for p in pre[i]])
        back = justify(sorted(range(1, n), key=lambda i: (-cur[i] - calls[i][4], -i)), after,
                       lambda p, i: calls[p][4] + calls[i][5] - calls[i][4] + delay(i, p) + MARGIN * (calls[p][0] == "R"))
        cur = justify(sorted(range(1, n), key=lambda i: (-back[i] - calls[i][4], i)), pre, lambda p, i: calls[p][5] + delay(p, i))
        if span(cur) < span(start):
            start = cur
    order = sorted(range(1, n), key=lambda i: (start[i] if calls[i][6] or calls[i][3] != 16 else -1.0, i))
    closes.update(max(grp, key=lambda i: (start[i], i)) for grp in groups)
    cnt, tok, seen, snap, issued = {}, {}, {q: {} for q in Q}, {}, {}
    for i in order:
        if calls[i][0] == "R":
            tok[i], snap[i] = (calls[i][2], calls[i][3]), {}
            cnt[calls[i][2]] = calls[i][3]
    for i in order:
        q, issue, sem, inc = calls[i][:4]
        if q == "R":
            continue
        for p in sorted(calls[i][6], key=lambda p: -start[p]):
            if q == calls[p][0] == "P" or (p, i) in loose:
                continue
            s, v = tok[p]
            if seen[q].get(s, 0) < v:
                for j in reversed(issued.get(s, [])):
                    if tok[j][1] <= v or start[j] + calls[j][5] + DONE <= start[i]:
                        p, v = (j, tok[j][1]) if tok[j][1] > v else (p, v)
                        break
                Q[q].wait_ge(T.sem[s], v)
                seen[q][s] = v
                for s2, v2 in snap[p].items():
                    seen[q][s2] = max(seen[q].get(s2, 0), v2)
        issue()
        cnt[sem] = cnt.get(sem, 0) + inc
        tok[i], snap[i] = (sem, cnt[sem]), dict(seen[q])
        if sem == "c" + q:
            issued.setdefault(sem, []).append(i)
    for sem, v in sorted(cnt.items()):
        if seen["G"].get(sem, 0) < v:
            g.wait_ge(T.sem[sem], v)
